import numpy as np, ml_dtypes
CORES = [9,25,41,57]
N = 4
BF = ml_dtypes.bfloat16
C, I, P, T, ST = 4096, 256, 1024, 4, 1
SX, SP = 16, 4
def parts(rng):
    return rng.integers(0, 256, (N, 8, C, 16)), rng.integers(0, 4096, (N, 8, I, 16)), rng.integers(0, 4096, (N, 8, P, 16)), rng.integers(1, 256, (N, 8, 16))
def turn(a):
    return np.ascontiguousarray(np.swapaxes(a, 2, 3)).reshape(N, 128, -1)
def pack(x, w, p, t):
    return {"xt": turn(x).astype(np.float32).astype(BF), "wd": turn(w).astype(np.int32), "pd": turn(p).astype(np.int32), "wt": np.reshape(t, (N, 128, 1)).astype(np.int32)}
def place(a, b, s):
    return ((a * b >> 5) + 37 * a + b + s) & (C - 1)
def setup_inputs(rng):
    x, w, p, t = parts(rng)
    return pack(x, w, p, t)
def setup_inputs_spread(rng):
    x, w, p, t = parts(rng)
    s = rng.choice(np.array([0.0, 0.25, 0.5, 1.0]), (N, 8, 1, 1))
    x = (x * np.exp2(-8 * s * rng.random((N, 8, C, 1)))).astype(np.int64)
    w = np.where(rng.random((N, 8, I, 1)) < 0.5, np.exp2(12 * rng.random(w.shape)).astype(np.int64) - 1, w)
    p = np.where(rng.random((N, 8, P, 1)) < 0.5, np.exp2(12 * rng.random(p.shape)).astype(np.int64) - 1, p)
    t = np.minimum(np.exp2(8 * rng.random(t.shape)).astype(np.int64), 255)
    return pack(x, np.minimum(w, 4095), np.minimum(p, 4095), t)
def setup_inputs_ends(rng):
    x, w, p, t = parts(rng); m = np.arange(16); s = np.arange(32)
    x = np.where(x < 128, 0, 255); x = np.where(rng.random(x.shape) < 0.1, np.abs(x - 1), x)
    x[:, :, (s - 1) & (C - 1)] = 0; x[:, :, (s + 37 * 4095) & (C - 1)] = 255
    w = np.where(rng.random((N, 8, I, 1)) < 0.75, 4095 * rng.integers(0, 2, w.shape), w)
    kind = rng.integers(0, 4, (N, 8, P, 1))
    p = np.where(kind == 0, 0, np.where(kind == 1, 4095, np.where(kind == 2, 4095 * rng.integers(0, 2, p.shape), p)))
    v = rng.integers(64, 2000, (N, 8))
    w[:, :, I - 1] = 0; w[:, :, I - 1, 14] = v; w[:, :, I - 1, 15] = 4095
    w[:, :, I - 2] = 4095; w[:, :, I - 2, 0] = 0; w[:, :, I - 2, 1] = v
    w[:, :, 0] = 0; w[:, :, 0, 15] = 4095; w[:, :, 1] = 4095 * (m % 2)
    p[:, :, 0] = 4095; p[:, 1::2, 0, 15] = 0
    t = np.where(t < 128, 1, 255); t[:, 0] = 1; t[:, 7] = 255
    return pack(x, w, p, t)
def setup_inputs_corners(rng):
    x, w, p, t = parts(rng); m = np.arange(16)
    kw = rng.integers(0, 6, (N, 8, I, 1)); z = rng.integers(0, 16, (N, 8, I, 1)); one = w[..., :1]
    w = np.where(kw == 0, one, np.where(kw == 1, w[..., m % 2], np.where(kw == 2, (one & 1023) + 1024 * (w & 3), np.where(kw == 3, np.where(m == z, w[..., 1:2], one), np.where(kw == 4, w[..., m % 8], w)))))
    kp = rng.integers(0, 4, (N, 8, P, 1))
    p = np.where(kp == 0, p[..., :1], np.where(kp == 1, p[..., m % 4], np.where(kp == 2, 4095 * (p & 1), p)))
    p[:, 1::2, ::SP] = w[:, 1::2]
    x[:, 0::4] = x[:, 0::4] & 1; x[:, 1::4] = x[:, 1::4][:, :, (np.arange(C) >> 2) & 7]; x[:, 2::4] = 255 * (x[:, 2::4] & 1)
    t[:, 0] = 1; t[:, 1] = 255; t[:, 2] = np.where(m == 15, 255, 1); t[:, 3] = np.where(m == 0, 1, 255)
    return pack(x, w, p, t)
def setup_inputs_crowd(rng):
    x, w, p, t = parts(rng); g1 = int(rng.integers(0, 8))
    for q in (0, 1, N - 1):
        for g in range(8):
            but = (g == g1) if q == 1 else (q > 1 and rng.random() < 0.5)
            base = rng.integers(0, 256, 16); x[q, g] = base
            if but:
                a = w[q, g]; b = np.roll(a, -1, axis=1)
                n = np.bincount(np.concatenate([place(a, b, 0).ravel(), place(b, a, 0).ravel()]), minlength=C)
                x[q, g, int(rng.choice(np.flatnonzero(n == 1)))] = 255 - base
    al = np.argsort(rng.random((8, 4096)), axis=1)[:, :4]
    a = np.take_along_axis(al, rng.integers(0, 4, (8, I)), 1)[:, :, None]; b = (a + rng.integers(1, C // 4, (8, I, 1))) & 4095
    w[2] = np.where(np.arange(16) == rng.integers(0, 16, (8, I, 1)), b, a)
    p[2, :, :, :4] = al[:, None, :]; p[2] = np.take_along_axis(p[2], np.argsort(rng.random((8, P, 16)), axis=2), 2)
    return pack(x, w, p, t)
def setup_inputs_brink(rng):
    x, w, p, t = parts(rng); m = np.arange(16)
    for q in range(N):
        for g in range(8):
            s = 1 + rng.permutation(36)
            cut = np.zeros(36, np.int64); cut[8:12] = 1
            if g % 2 == 0:
                cut[12:] = rng.integers(2, 256, 24); cut[35] = 255
            else:
                cut[12:24] = 2040; cut[24:] = 2041
            o = np.argsort(rng.random((36, 16)), axis=1)
            far = 255 - np.clip(cut[:, None] - 255 * o, 0, 255)
            lo = (255 - far) * rng.integers(0, 2, (36, 16)); up = rng.random((36, 16)) < 0.5
            x[q, g, s] = np.where(up, lo + far, lo); x[q, g, 37 * s] = np.where(up, lo, lo + far)
            p[q, g] = s[rng.integers(0, np.where(rng.random((P, 1)) < 0.5, 24, 36), (P, 16))]
            z1 = rng.integers(1, 7, (I, 1)); z2 = z1 + 2 + rng.integers(0, 8, (I, 1))
            v = np.where(m == z1, s[rng.integers(8, 12, (I, 1))], np.where(m == z2, s[rng.integers(0, 8, (I, 1))], 0))
            w[q, g] = np.where(rng.random((I, 1)) < 0.75, v, w[q, g])
    return pack(x, w, p, t)
def check_inputs(d):
    bad = []
    for k, lo, hi in (("xt", 0, 255), ("wd", 0, 4095), ("pd", 0, 4095), ("wt", 1, 255)):
        a = np.asarray(d[k]).astype(np.float64)
        if not (np.all(a >= lo) and np.all(a <= hi) and np.all(a == np.floor(a))): bad.append("range of " + k)
    return bad
def reference(xt, wd, pd, wt):
    x = np.ascontiguousarray(np.swapaxes(xt.astype(np.float32).astype(np.int32).reshape(N, 8, 16, C), 2, 3))
    w = np.ascontiguousarray(np.swapaxes(wd.astype(np.int64).reshape(N, 8, 16, I), 2, 3))
    p = np.ascontiguousarray(np.swapaxes(pd.astype(np.int64).reshape(N, 8, 16, P), 2, 3))
    wts = wt.astype(np.int64).reshape(N, 8, 1, 16)
    gi = np.arange(8)[:, None]; ti = np.arange(I)[None, :]; g3 = np.arange(8)[:, None, None]
    A = np.zeros(N, np.int64)
    for t in range(T):
        A2 = np.zeros(N, np.int64)
        for r in range(N):
            q = (r + ST * t) % N
            v = w[r].copy(); v1 = np.roll(v, -1, axis=2)
            f = x[q][g3, place(v, v1, A[q])]; h = x[q][g3, place(v1, v, A[q])]
            e = np.add.reduce(np.abs(f - h), axis=3)
            k = np.argmax(e, axis=2); kn = (k + 1) & 15
            c = np.where(e[gi, ti, (k - 1) & 15] >= e[gi, ti, kn], k, kn)
            u = np.add.reduce(wts[q] * f[gi, ti, k], axis=2)
            b = p[q][gi, u & (P - 1)]
            before = v[gi, ti, (c - 1) & 15][:, :, None]; after = v[gi, ti, (c + 1) & 15][:, :, None]
            y = x[q][g3, place(before, b, A[q])]; z = x[q][g3, place(b, after, A[q])]
            E = np.add.reduce(np.abs(y - z), axis=3)
            j = np.argmin(E, axis=2)
            good = 2 * E[gi, ti, j] < e[gi, ti, k]
            mend = v.copy(); mend[gi, ti, c] = b[gi, ti, j]
            swap = v.copy(); swap[gi, ti, k] = v[gi, ti, kn]; swap[gi, ti, kn] = v[gi, ti, k]
            new = np.where(good[:, :, None], mend, swap)
            gg, ii = np.nonzero(good)
            p[q, gg, SP * ii + (u[gg, ii] & (SP - 1))] = new[gg, ii]
            x[q, gi, SX * ti + (u & (SX - 1))] = (y[gi, ti, j] + z[gi, ti, j]) >> 1
            w[r] = new; A2[q] = (8 * I - len(gg)) & 31
        A = A2
    return {"yw": turn(w).astype(np.float32), "yp": turn(p).astype(np.float32), "yx": turn(x).astype(np.float32).astype(BF)}

@@ -1,0 +1,472 @@
+from concourse.mybir import AluOpType as A, ActivationFunctionType as F, AxisListType as AX
+
+NV = 4
+W16 = "float16"
+PLAN = {
+    "10": [(512, "v"), (512, "v"), (512, "v"), (512, "v")],
+    "11": [(512, "s"), (512, "s"), (512, "v"), (512, "v")],
+    "20": [(512, "s"), (512, "s"), (512, "v"), (512, "v")],
+    "21": [(512, "s"), (512, "v"), (512, "v"), (512, "v")],
+}
+PERIOD = 400
+ORDER = {
+    'out':[401,456,517,479,457],'wL':[253,257,259,262,264,402,431,267,268,269,432,478],'i11':[3,18,19,20,21],'x0':[250,404],'f10':[5,6,8,10],
+    'c1':[-288,-273,-213,-100,-102,-354,-324,-232,-164,-160,-124,-372,-353,-351,-350,-252,-184,-249,-323,-205,-162,-173,-111,-174,-204,-348,-112,-103,-274,-270,-189,-106,-286,-285,-266,-221,-219,-224,-222,-300,-223,-218,-235,-163,-220,-278,-209,-271,-269,-254,-253,40,-212,25,11,-199,26,9,7,24,-117],
+    'o0':[-104,12],'d10':[13,14,15,17],'c0':[-308,-309,-558,-347,-287,-384,-330,-339,-306,-293,-296,-284,-251,-272,-200,-245,-190],'o1':[22],'c2':[23,44],
+    's10':[27,37,41,39,42,58,43,60,65,59,62,66,67,80,85,68,86,81,82,96,88,102,103,106,89,90,93],'a10':[29,30,33,34],'wr1':[35,36],'st1':[438],
+    'f11':[55,54,48,45,72,51],'pp0':[63,84,101,97,105,172,110,202,212,154],'a11':[71,74,64,75,95,73],'d11':[87,69],
+    's11':[83,98,99,109,132,133,135,136,138,137,140,142,141,150,153,144,157,156,159,161,174,171,173,175,186,190,194],'f20':[123,108,121,111,118,125],
+    'r0':[119,169,193,204,206,208,217,234,243,249,213,247],'sw0':[120,124],'d20':[139,158],'a20':[145,166,143,164,163,167],
+    'pp1':[152,160,185,183,184,170,189,192,215,246],'sw1':[162,197],'f21':[228,225,199,198,224],'w0':[203,205,209,214,219,223,232,218,220,222,244,245],
+    'd21':[221,207,229],'a21':[231,239,233,230,241],'r1':[235,251,252,254,255,260,263,266,275,278,265,272],'st0':[248],
+    'w1':[256,258,261,270,273,281,290,271,274,279,291,301],'i10':[-123,-120,-113,-114,-107],'cnt':[282,292,295],'wr0':[-116,-101],'x1':[285]}
+
+SCRATCH = {
+    "X": ("sbuf", [128, 4128], "bfloat16"),
+    "ST": ("sbuf", [128, 1152], "float32"),
+    "wdi": ("sbuf", [128, 256], "int32"),
+    "pdi": ("sbuf", [128, 1024], "int32"),
+    "wti": ("sbuf", [128, 8], "int32"),
+    "wtf": ("sbuf", [128, 8], "float32"),
+    "Ac": ("sbuf", [128, 8], "float32"),
+    "Aq": ("sbuf", [128, 8], "int32"),
+    "val": ("sbuf", [128, 128], "float32"),
+    "gv": ("sbuf", [128, 256], "float32"),
+    "CW": ("sbuf", [128, 11 * 128], W16),
+    "Ib": ("sbuf", [128, 512], "bfloat16"),
+    "If": ("sbuf", [128, 256], "float32"),
+    "G8": ("sbuf", [128, 32], "float32"),
+    "RK": ("sbuf", [128, 40], "bfloat16"),
+    "DGi": ("sbuf", [128, 128], "int32"),
+    "DG": ("sbuf", [128, 256], "bfloat16"),
+    "IM": ("sbuf", [128, 128], "int32"),
+    "Li": ("sbuf", [128, 32], "int32"),
+    "L": ("sbuf", [128, 32], "uint16"),
+    "STEP": ("sbuf", [128, 128], "float32"),
+    "rowf": ("sbuf", [128, 128], "float32"),
+    "row": ("sbuf", [128, 1024], "bfloat16"),
+}
+for _h in range(2):
+    for _n, _c, _d in (
+        ("F", 2048, "bfloat16"), ("D", 2048, "bfloat16"), ("AD", 2048, "bfloat16"),
+        ("O1", 256, "uint16"), ("O2", 256, "uint16"), ("OS", 40, "uint16"),
+        ("I1", 256, "int32"), ("I2", 256, "int32"), ("P1", 128, "float32"), ("P2", 256, "float32"),
+        ("Wr", 384, "float32"), ("MK", 384, W16), ("B", 128, W16), ("OH", 128, "bfloat16"),
+        ("S1", 384, "float32"), ("S2", 256, "float32"), ("NF", 128, "float32"), ("XD", 384, "float32"),
+        ("XM", 128, "float32"), ("SW", 384, "float32"), ("TP", 32, "int32"), ("CI", 104, "int32"),
+        ("AB", 40, "int32"), ("C3", 24, "int32"), ("NG", 24, "float32"), ("G1", 128, "float32"), ("RI", 128, "int32"),
+        ("Wl", NV * 128, W16), ("Wo", NV * 128, W16), ("Yl", 128, "float32"), ("Yo", 128, "float32"),
+    ):
+        SCRATCH["%s%d" % (_n, _h)] = ("sbuf", [128, _c], _d)
+    for _b in range(4):
+        SCRATCH["b%d%d" % (_b, _h)] = ("psum", [128, 512], "float32")
+SEMAPHORES = ["v", "s", "t", "g", "sent"] + ["d%d" % i for i in range(10)] + ["arr%d" % i for i in range(2 * NV)]
+
+CYC, FIX, HOP, PEC, GAT, SCA, DMA, FAR = 1.0, 60.0, 90.0, 0.55, 1.56, 3.8, 2200.0, 3200.0
+
+
+def v(name, lo, hi, st=1, p=128):
+    return (name, lo, hi, st, p)
+
+
+def width(x):
+    return (x[2] - x[1] + x[3] - 1) // x[3]
+
+
+def build(g, T, nxt):
+    ops = []
+    now = [(0, "c0")]
+
+    def at(t, key):
+        now[0] = (t, key)
+
+    def ap(x):
+        return T[x[0]][0:x[4], x[1]:x[2]:x[3]] if x[3] > 1 else T[x[0]][0:x[4], x[1]:x[2]]
+
+    def ind(win, off):
+        return ap(win).indirect(ap(off))
+
+    def add(q, fn, rd, wr, t, kind=None):
+        ops.append((q, fn, [r for r in rd if isinstance(r, tuple)], wr, t, kind, now[0]))
+
+    def sc(x):
+        return ap(x) if isinstance(x, tuple) else x
+
+    def cost(n, r=1.0):
+        return FIX + CYC * max(50.0, n * r)
+
+    V = g.vector
+
+    def tt(o, a, b, op, off=None):
+        two = SCRATCH[a[0]][0] != "psum" and SCRATCH[b[0]][0] != "psum"
+        add("v", lambda: V.tensor_tensor(ap(o), ind(a, off) if off else ap(a), ap(b), op), [a, b, off], [o],
+            cost(width(o), GAT if off else 2.0 if two else 1.0))
+
+    def ts(o, a, s1, s2, op0, op1=None, off=None):
+        def fn():
+            x = ind(a, off) if off else ap(a)
+            if op1 is None:
+                return V.tensor_scalar(ap(o), x, sc(s1), None, op0)
+            return V.tensor_scalar(ap(o), x, sc(s1), sc(s2), op0, op1)
+        add("v", fn, [a, s1, s2, off], [o], cost(width(o), GAT if off else 1.0))
+
+    def cp(o, a, off=None):
+        add("v", lambda: V.tensor_copy(ap(o), ind(a, off) if off else ap(a)), [a, off], [o], cost(width(o), GAT if off else 1.0))
+
+    def scan(o, d0, d1, op0, op1):
+        add("v", lambda: V.tensor_tensor_scan(ap(o), ap(d0), ap(d1), 0.0, op0, op1), [d0, d1], [o], cost(width(o)))
+
+    def act(o, a, fn, off=None, bias=0.0, scale=1.0):
+        add("s", lambda: g.scalar.activation(ap(o), ind(a, off) if off else ap(a), fn, bias=bias, scale=sc(scale)), [a, off, scale], [o],
+            cost(width(o), GAT if off else 1.0))
+
+    def mm(group):
+        def fn():
+            last = None
+            for o, l, r, s0, s1 in group:
+                last = g.tensor.matmul(ap(o), ap(l), ap(r), s0, s1)
+            return last
+        t = sum(15.0 + PEC * max(min(64, width(l)), width(r)) * (4 if SCRATCH[l[0]][2] == "float32" else 1) for o, l, r, s0, s1 in group)
+        add("t", fn, [x[1] for x in group] + [x[2] for x in group], [x[0] for x in group], 60.0 + t)
+
+    def iota(o, pat, base, cm):
+        flt = SCRATCH[o[0]][2] != "int32"
+        add("g", (lambda: g.iota(ap(o), pat, base, cm, allow_small_or_imprecise_dtypes=True)) if flt else (lambda: g.iota(ap(o), pat, base, cm)),
+            [], [o], 130.0 + 2 * CYC * width(o))
+
+    def dma(q, o, a, rd, wr, t, **kw):
+        eng = {"y": g.sync, "s": g.scalar, "g": g}[q]
+        add(q, lambda: eng.dma_start(o, a, **kw), rd, wr, t, "dma")
+
+    I16, NI16, SM, SP, NL, NR, LF, LG, GG, G3232, G2080 = [v("CW", 128 * i, 128 * i + 128) for i in range(11)]
+    IB, IBN, IBM, IB2 = [v("Ib", 128 * i, 128 * i + 128) for i in range(4)]
+    IF, ONES = v("If", 0, 128), v("If", 128, 256)
+    ONE, M16, ROW1, ROW2, ROW3 = v("row", 0, 128, 1, 1), v("row", 128, 256, 1, 1), v("row", 256, 512, 1, 1), v("row", 512, 768, 1, 1), v("row", 768, 1024, 1, 1)
+    L15, LB, STEP, Ac = v("L", 0, 16), v("L", 16, 24), v("STEP", 0, 128), v("Ac", 0, 1)
+
+    dma("y", T.wdi[:], T.wd[:], [], [v("wdi", 0, 256)], DMA)
+    dma("y", T.X[:, 0:2048], T.xt[:, 0:2048], [], [v("X", 0, 2048)], DMA + 3500)
+    dma("s", T.X[:, 2048:4096], T.xt[:, 2048:4096], [], [v("X", 2048, 4096)], DMA + 3500)
+    dma("g", T.wti[:, 0:1], T.wt[:], [], [v("wti", 0, 1)], DMA + 1500, allow_slow_non_contiguous=True)
+    dma("y", T.pdi[:], T.pd[:], [], [v("pdi", 0, 1024)], DMA + 5000)
+
+    val, gv, gm = v("val", 0, 128), v("gv", 0, 128), v("gv", 128, 256)
+    iota(val, [[-1, 128]], 0, 1)
+    ts(I16, val, 0.0, None, A.is_equal)
+    ts(SP, val, 1.0, None, A.is_equal)
+    ts(v("CW", SP[1] + 15, SP[2], 16), v("val", 15, 128, 16), -15.0, None, A.is_equal)
+    ts(NL, SP, 2080.0, None, A.mult)
+    ts(NR, I16, 3232.0, None, A.mult)
+    tt(LF, NL, NR, A.add)
+    ts(NL, SP, 3232.0, None, A.mult)
+    ts(NR, I16, 2080.0, None, A.mult)
+    tt(LG, NL, NR, A.add)
+    for h in range(2):
+        ts(v("Wl%d" % h, 0, 128), v("wdi", 128 * h, 128 * h + 128), -2048.0, None, A.add)
+    at(0, "c1")
+    ts(NI16, val, 0.0, -1.0, A.is_equal, A.mult)
+    ts(SM, val, -1.0, None, A.is_equal)
+    ts(v("CW", SM[1], SM[2], 16), v("val", 0, 128, 16), 15.0, None, A.is_equal)
+    tt(NL, I16, SP, A.subtract)
+    tt(NR, I16, SM, A.subtract)
+    act(IF, val, F.Abs)
+    act(IF, IF, F.Relu, bias=1.0, scale=-1.0)
+    for o, c in ((IB, 1.0), (IBN, -2048.0), (IBM, -1.0), (IB2, 2.0)):
+        act(o, IF, F.Identity, scale=c)
+    iota(gv, [[-32, 8], [0, 16]], -15, 2)
+    act(gv, gv, F.Abs)
+    act(gm, gv, F.Sign, bias=16.0, scale=-1.0)
+    act(gm, gm, F.Relu)
+    cp(GG, gm)
+    ts(G3232, gm, 3232.0, None, A.mult)
+    ts(G2080, gm, 2080.0, None, A.mult)
+    g8 = v("gv", 128, 256, 16)
+    for j in range(4):
+        act(v("G8", 8 * j, 8 * j + 8), g8, F.Identity, scale=1.0 if j < 2 else -1.0)
+    cp(v("wtf", 0, 1), v("wti", 0, 1))
+    for j, c in enumerate((16.0, -1.0, 1.0, -2048.0, v("wtf", 0, 1))):
+        act(v("RK", 8 * j, 8 * j + 8), g8, F.Identity, scale=c)
+    iota(v("DGi", 0, 128), [[0, 8], [-1, 16]], 16, 1)
+    ts(v("DGi", 0, 128), v("DGi", 0, 128), 15, None, A.bitwise_and)
+    ts(v("DG", 0, 128), v("DGi", 0, 128), 0.0, None, A.is_equal)
+    act(v("DG", 128, 256), v("DG", 0, 128), F.Copy)
+    iota(v("Li", 0, 16), [[16, 16]], 15, 0)
+    iota(v("Li", 16, 24), [[1, 8]], 0, 0)
+    cp(v("L", 0, 24), v("Li", 0, 24))
+    iota(STEP, [[0, 128]], 1, 0)
+    iota(v("STEP", 0, 128, 16), [[0, 8]], -16000000, 0)
+    iota(v("IM", 0, 128), [[0, 8], [1, 16]], 0, 0)
+    iota(ONES, [[0, 128]], 1, 0)
+    r15 = v("rowf", 0, 128, 1, 1)
+    iota(r15, [[0, 8], [-1, 16]], 15, 0)
+    iota(ONE, [[0, 128]], 1, 0)
+    iota(M16, [[-16, 128]], 0, 0)
+    act(v("row", 256, 384, 1, 1), r15, F.Identity, bias=4096.0, scale=8192.0)
+    act(v("row", 384, 512, 1, 1), r15, F.Identity, scale=1048576.0)
+    iota(v("row", 512, 640, 1, 1), [[0, 128]], 0, 0)
+    act(v("row", 640, 768, 1, 1), r15, F.Identity, bias=2048.0, scale=4096.0)
+    iota(ROW3, [[1152, 2], [0, 128]], 2080, 0)
+    TI = v("CI0", 0, 8)
+    iota(TI, [[0, 8]], 0, 1)
+    ts(TI, TI, 15, None, A.bitwise_and)
+    iota(v("CI0", 8, 16), [[16, 8]], 0, 0)
+    tt(TI, TI, v("CI0", 8, 16), A.add)
+    for h in range(2):
+        cp(v("AB%d" % h, 0, 8), TI)
+        ts(v("AB%d" % h, 32, 40), TI, 1024.0, None, A.add)
+        ts(v("C3%d" % h, 0, 8), TI, 4.0, 512.0 * h, A.mult, A.add)
+        ts(v("C3%d" % h, 8, 16), TI, 16.0, None, A.mult)
+        ts(v("C3%d" % h, 16, 24), TI, 128.0, None, A.add)
+    at(0, "c2")
+    cp(v("ST", 0, 1024), v("pdi", 0, 1024))
+    iota(v("ST", 1024, 1152), [[0, 128]], 0, 0)
+
+    def names(h):
+        return lambda n, lo, hi, st=1: v("%s%d" % (n, h), lo, hi, st)
+
+    def numbers(o, i, t):
+        if t:
+            ts(o, i, Ac, None, A.add)
+        else:
+            cp(o, i)
+
+    def gathers(t, h, step):
+        u = names(h)
+        Xw = v("X", 0, 4128 if t else 4096)
+        key = "%d%d" % (step, h)
+        off, lo, n = "O%d" % step, 0, 0
+        for size, who in PLAN[key]:
+            hi = lo + size
+            o1, o2 = u(off, lo // 16, hi // 16), u(off, 128 + lo // 16, 128 + hi // 16)
+            at(t, "f" + key)
+            if who == "s":
+                act(u("F", lo, hi), Xw, F.Identity, off=o1, scale=1.0 / step)
+                act(u("D", lo, hi), Xw, F.Copy, off=o2)
+                at(t, "a" + key)
+                for s in range(lo, hi, 512):
+                    e = min(hi, s + 512)
+                    bank = u("b3" if n % 2 == 0 else "b1", 0, e - s)
+                    n += 1
+                    mm([(bank, IB if step == 1 else IB2, u("F", s, e), True, False), (bank, IBM, u("D", s, e), False, True)])
+                    act(u("AD", s, e), bank, F.Abs)
+            else:
+                act(u("F", lo, hi), Xw, F.Copy, off=o1)
+                at(t, "d" + key)
+                tt(u("D", lo, hi), Xw, u("F", lo, hi), A.subtract, off=o2)
+                at(t, "a" + key)
+                act(u("AD", lo, hi), u("D", lo, hi), F.Abs)
+            lo = hi
+
+    def step1(t, h):
+        u = names(h)
+        W = u("Wl", 128 * t, 128 * t + 128)
+        at(t, "i1%d" % h)
+        mm([(u("b1", 256, 384), SP, W, True, True), (u("b2", 0, 128), LF, W, True, True), (u("b2", 128, 256), LG, W, True, True)])
+        tt(u("P1", 0, 128), u("b1", 256, 384), W, A.mult)
+        tt(u("I1", 0, 128), u("b2", 0, 128), u("P1", 0, 128), A.add)
+        tt(u("I1", 128, 256), u("b2", 128, 256), u("P1", 0, 128), A.add)
+        ts(u("I1", 0, 256), u("I1", 0, 256), 5, 4095, A.arith_shift_right, A.bitwise_and)
+        at(t, "o%d" % h)
+        for lo, hi in ((0, 128), (128, 256)) if h == 0 else ((0, 256),):
+            numbers(u("O1", lo, hi), u("I1", lo, hi), t)
+        at(t, "wr%d" % h)
+        mm([(u("b1", 0, 128), SM, W, True, True), (u("b1", 128, 256), NI16, W, True, True)])
+        act(u("Wr", 0, 384), u("b1", 0, 384), F.Copy)
+        gathers(t, h, 1)
+        at(t, "s1%d" % h)
+        mm([(u("b2", 0, 256), ONE, ROW1, True, False)] +
+           [(u("b2", 128 + k, 256, 16), u("F", k, 2048, 16), v("RK", 32, 40), False, False) for k in range(16)])
+        a = [u("AD", k, 2048, 16) for k in range(16)]
+        mm([(u("b0", k, 128, 16), a[k], v("RK", 0, 8), True, True) for k in range(16)])
+        mm([(u("b2", (k + d) % 16, 128, 16), a[k], v("RK", 12 + 4 * d, 20 + 4 * d), False, k == 15 and d == 1) for k in range(16) for d in (-1, 1)])
+        scan(u("S1", 256, 384), STEP, u("b0", 0, 128), A.add, A.max)
+        tt(u("NF", 0, 128), u("b0", 0, 128), u("S1", 256, 384), A.not_equal)
+        scan(u("S1", 0, 128), u("NF", 0, 128), u("b2", 128, 256), A.mult, A.max)
+        scan(u("S1", 128, 256), u("NF", 0, 128), u("b2", 0, 128), A.mult, A.max)
+        tt(u("XD", 0, 128), u("S1", 0, 128), v("DG", 0, 128), A.mult, off=v("L", 0, 8))
+        mm([(u("b0", 384, 392), u("XD", 0, 128), v("G8", 0, 8), True, True)])
+        ts(u("TP", 0, 8), u("S1", 128 + 15, 256, 16), -1.0 / 8192, 16.0 - 2.0 ** -14, A.mult, A.add)
+        ts(u("TP", 8, 16), u("TP", 0, 8), 15, None, A.bitwise_and)
+        tt(u("OH", 0, 128), u("TP", 8, 16), v("IM", 0, 128), A.is_equal, off=LB)
+        cp(u("CI", 0, 8), u("b0", 384, 392))
+        ts(u("CI", 16, 24), u("CI", 0, 8), 1023, None, A.bitwise_and)
+        cp(u("OS", 0, 8), u("CI", 16, 24))
+        mm([(u("b2", 128 * j, 128 * j + 128), u("OH", 0, 128), IB, True, True) for j in range(3)])
+        ts(u("B", 0, 128), v("ST", 0, 1024), -2048.0, None, A.add, off=u("OS", 0, 8))
+        tt(u("MK", 0, 384), u("b2", 0, 384), u("Wr", 0, 384), A.mult)
+
+    def step2(t, h):
+        u = names(h)
+        W = u("Wl", 128 * t, 128 * t + 128)
+        ma, mp, mb = u("MK", 0, 128), u("MK", 128, 256), u("MK", 256, 384)
+        at(t, "s1%d" % h)
+        mm([(u("b1", 256, 384), G3232, ma, True, True), (u("b1", 384, 512), G2080, mb, True, True),
+            (u("b1", 0, 256), ONE, ROW3, True, False), (u("b1", 0, 128), GG, ma, False, False), (u("b1", 128, 256), GG, mb, False, True)])
+        tt(u("P2", 0, 128), u("b1", 0, 128), u("B", 0, 128), A.mult)
+        tt(u("P2", 128, 256), u("b1", 128, 256), u("B", 0, 128), A.mult)
+        for lo, hi in ((0, 128), (128, 256)):
+            tt(u("I2", lo, hi), u("b1", 256 + lo, 256 + hi), u("P2", lo, hi), A.add)
+            ts(u("I2", lo, hi), u("I2", lo, hi), 5, 4095, A.arith_shift_right, A.bitwise_and)
+            numbers(u("O2", lo, hi), u("I2", lo, hi), t)
+        at(t, "sw%d" % h)
+        mm([(u("b3", 128, 256), I16, W, True, False), (u("b3", 128, 256), NL, ma, False, False), (u("b3", 128, 256), NL, mp, False, True),
+            (u("b3", 256, 384), I16, W, True, False), (u("b3", 256, 384), NR, mb, False, False), (u("b3", 256, 384), NR, mp, False, True)])
+        act(u("SW", 128, 384), u("b3", 128, 384), F.Copy)
+        at(t, "pp%d" % h)
+        tt(u("XD", 128, 384), u("S1", 128, 384), v("DG", 0, 256), A.mult, off=L15)
+        mm([(u("b2", 392, 400), u("XD", 128, 256), v("G8", 0, 8), True, True), (u("b2", 400, 416), u("XD", 256, 384), v("G8", 0, 16), True, True)])
+        cp(u("CI", 8, 16), u("b2", 392, 400))
+        ts(u("CI", 24, 40), u("b2", 400, 416), 1.0 / 32, 1.0 / 64, A.mult, A.add)
+        ts(u("CI", 40, 48), u("CI", 0, 8), 3, None, A.bitwise_and)
+        ts(u("CI", 48, 56), u("CI", 0, 8), 15, None, A.bitwise_and)
+        ts(u("CI", 56, 64), u("CI", 8, 16), 5, 128, A.arith_shift_right, A.bitwise_and)
+        tt(u("AB", 8, 32), u("CI", 40, 64), u("C3", 0, 24), A.add)
+        cp(u("OS", 16, 24), u("AB", 16, 24))
+        ts(u("CI", 24, 40), u("CI", 24, 40), 2048.0, None, A.mult)
+        gathers(t, h, 2)
+        at(t, "r%d" % h)
+        mm([(u("b0", 0, 256), ONE, ROW2, True, False), (u("b0", 0, 128), M16, ONE, False, False), (u("b0", 128, 256), u("B", 0, 128), I16, False, False)])
+        mm([(u("b0", k, 128, 16), u("AD", k, 2048, 16), v("RK", 24, 32), False, k == 15) for k in range(16)])
+        scan(u("S2", 0, 128), STEP, u("b0", 0, 128), A.add, A.max)
+        tt(u("XD", 0, 128), u("S2", 0, 128), v("DG", 0, 128), A.mult, off=v("L", 0, 8))
+        mm([(u("b2", 416, 432), u("XD", 0, 128), v("G8", 16, 32), True, True)])
+        ts(u("CI", 64, 80), u("b2", 416, 432), 15.0, None, A.add)
+        ts(u("CI", 80, 88), u("CI", 64, 72), 2047, None, A.bitwise_and)
+        cp(u("OS", 8, 16), u("CI", 80, 88))
+        act(u("G1", 0, 128), u("D", 0, 2048), F.Identity, off=u("OS", 8, 16), bias=-0.25, scale=0.5)
+        tt(u("RI", 0, 128), u("F", 0, 2048), u("G1", 0, 128), A.add, off=u("OS", 8, 16))
+        tt(u("NG", 0, 16), u("CI", 64, 80), u("CI", 24, 40), A.is_ge)
+        if t < NV - 1:
+            add("v", lambda: V.tensor_reduce(ap(u("NG", 16, 17)), ap(u("NG", 0, 8)), AX.X, A.add), [u("NG", 0, 8)], [u("NG", 16, 17)], cost(8))
+        at(t, "wL" if t == NV - 1 and h else "w%d" % h)
+        tt(u("NF", 0, 128), u("b0", 0, 128), u("S2", 0, 128), A.not_equal)
+        scan(u("S2", 128, 256), u("NF", 0, 128), u("b0", 128, 256), A.mult, A.max)
+        cp(u("TP", 16, 24), u("S2", 128 + 15, 256, 16))
+        ts(u("TP", 24, 32), u("TP", 16, 24), 4095, None, A.bitwise_and)
+        tt(u("XM", 0, 128), u("TP", 24, 32), u("OH", 0, 128), A.mult, off=LB)
+        mm([(u("b3", 0, 128), I16, W, True, False), (u("b3", 0, 128), I16, mp, False, False),
+            (u("b3", 0, 128), u("OH", 0, 128), IBN, False, False), (u("b3", 0, 128), u("XM", 0, 128), IF, False, True)])
+        act(u("SW", 0, 128), u("b3", 0, 128), F.Copy)
+        tt(u("CI", 88, 104), u("NG", 0, 16), u("AB", 24, 40), A.mult)
+        tt(u("CI", 88, 104), u("CI", 88, 104), u("AB", 0, 16), A.max)
+        cp(u("OS", 24, 40), u("CI", 88, 104))
+        if t < NV - 1:
+            src, dst = u("Wo", 128 * t, 128 * t + 128), u("Wl", 128 * t + 128, 128 * t + 256)
+            cp(src, u("SW", 0, 384), off=u("OS", 24, 32))
+        else:
+            src, dst = u("Yo", 0, 128), u("Yl", 0, 128)
+            act(src, u("SW", 0, 384), F.Identity, off=u("OS", 24, 32), bias=2048.0)
+        sem = T.sem["arr%d" % (2 * t + h)]
+        add("g", lambda: g.remote_dma(ap(dst), ap(src), sem, T.sem.sent, nxt[1], nxt[0], nxt[2]), [src], [dst], FAR, ("far", "arr%d" % (2 * t + h)))
+
+    def writes(t, h):
+        u = names(h)
+        at(t, "x%d" % h)
+        xw, o = v("X", 2048 * h, 2048 * h + 2048), u("OS", 16, 24)
+        add("v", lambda: V.tensor_copy(ind(xw, o), ap(u("RI", 0, 128))), [o, u("RI", 0, 128)], [xw], cost(128, SCA))
+        if h == 0 and t < NV - 1:
+            act(v("X", 4096, 4128), v("X", 0, 32), F.Copy)
+        at(t, "st%d" % h)
+        sw, o2 = v("ST", 0, 1152), u("OS", 32, 40)
+        add("v", lambda: V.tensor_scalar(ind(sw, o2), ap(u("SW", 0, 128)), 1.0, 2048.0, A.mult, A.add), [o2, u("SW", 0, 128)], [sw], cost(128, SCA))
+
+    for t in range(NV):
+        step1(t, 0)
+        step1(t, 1)
+        step2(t, 0)
+        step2(t, 1)
+        writes(t, 0)
+        writes(t, 1)
+        if t < NV - 1:
+            at(t, "cnt")
+            c = v("b21", 432, 433)
+            mm([(c, ONES, v("NG0", 16, 17), True, False), (c, ONES, v("NG1", 16, 17), False, True)])
+            ts(v("Aq", 0, 1), c, 1.0 / 32, -15.5 / 32, A.mult, A.add)
+            ts(Ac, v("Aq", 0, 1), -32.0, c, A.mult, A.add)
+    at(NV - 1, "out")
+    for h in range(2):
+        q = "ys"[h]
+        dma(q, T.yx[:, 2048 * h:2048 * h + 2048], T.X[:, 2048 * h:2048 * h + 2048], [v("X", 2048 * h, 2048 * h + 2048)], [], DMA + 2500)
+        dma("y", T.yw[:, 128 * h:128 * h + 128], T["Yl%d" % h][:], [v("Yl%d" % h, 0, 128)], [], DMA)
+    dma("y", T.yp[:], T.ST[:, 0:1024], [v("ST", 0, 1024)], [], DMA + 2500)
+    return ops
+
+
+def depend(ops):
+    seen = {}
+    deps = []
+    for i, o in enumerate(ops):
+        d = set()
+        acc = [(r, False) for r in o[2]] + [(r, True) for r in o[3]]
+        for r, w in acc:
+            ps = SCRATCH[r[0]][0] == "psum"
+            for j, lo, hi, w2 in seen.get(r[0], []):
+                if (ps and ops[j][0] != o[0]) or ((w or w2) and lo < r[2] and r[1] < hi):
+                    d.add(j)
+        for r, w in acc:
+            lst = seen.setdefault(r[0], [])
+            if w and r[3] == 1 and r[4] == 128 and SCRATCH[r[0]][0] != "psum":
+                lst[:] = [e for e in lst if not (r[1] <= e[1] and e[2] <= r[2])]
+            lst.append((i, r[1], r[2], w))
+        d.discard(i)
+        deps.append(sorted(d))
+    return deps
+
+
+def arrange(ops, deps):
+    nth, place = {}, []
+    for i, o in enumerate(ops):
+        t, key = o[6]
+        nth[o[6]] = nth.get(o[6], -1) + 1
+        x = PERIOD * t + ORDER[key][nth[o[6]]] if key in ORDER else -1000 + i
+        place.append(max([x] + [place[j] + 0.001 for j in deps[i]]))
+    return sorted(range(len(ops)), key=lambda i: (place[i], i))
+
+
+def rank_program(g, core, T, topo):
+    rank = T.rank_of(core)
+    if rank is None:
+        return
+    to = T.cores[(rank + 1) % len(T.cores)]
+    rid, pid = topo.addr(to)[0:2]
+    lanes = len(topo.engines(core, to))
+    ops = build(g, T, (rid, pid, topo.mask(core, to)))
+    deps = depend(ops)
+    order = arrange(ops, deps)
+    queue = {"v": g.vector, "s": g.scalar, "t": g.tensor, "g": g, "y": g.sync}
+    needed = set(j for i in order for j in deps[i] if not (ops[i][0] == "t" and ops[j][0] == "t"))
+    mark, count, nd, far = {}, {q: 0 for q in "vstg"}, 0, 0
+    waited = {q: {} for q in queue}
+    pos = {i: n for n, i in enumerate(order)}
+    know, direct = {}, {}
+    for i in order:
+        q, fn, rd, wr, t, kind, pr = ops[i]
+        for j in sorted(deps[i], key=lambda j: -pos[j]):
+            if j in mark and not (q == "t" and ops[j][0] == "t"):
+                s, n = mark[j]
+                if waited[q].get(s, 0) < n:
+                    queue[q].wait_ge(T.sem[s], n)
+                    waited[q][s] = n
+                    direct[s] = max(direct.get(s, 0), n)
+                    for s2, n2 in know[j].items():
+                        waited[q][s2] = max(waited[q].get(s2, 0), n2)
+        know[i] = dict(waited[q]) if kind is None or kind == "dma" else {}
+        x = fn()
+        if kind == "dma":
+            mark[i] = ("d%d" % nd, 16)
+            x.then_inc(T.sem["d%d" % nd], 16)
+            nd += 1
+        elif kind is not None:
+            mark[i] = (kind[1], lanes)
+            far += 1
+        elif i in needed:
+            count[q] += 1
+            mark[i] = (q, count[q])
+            x.then_inc(T.sem[q], 1)
+    g.wait_ge(T.sem.sent, far * lanes)
+    last = {}
+    for s, n in mark.values():
+        last[s] = max(last.get(s, 0), n)
+    for s in last:
+        if direct.get(s, 0) < last[s]:
+            g.wait_ge(T.sem[s], last[s])

@@ -1,106 +1,112 @@
-from concourse.mybir import AluOpType as A, ActivationFunctionType as F, AxisListType as AX
+import math
+
+from concourse.mybir import AluOpType as A, ActivationFunctionType as F
 
 NV = 4
 W16 = "float16"
-PLAN = {
-    "10": [(512, "v"), (512, "v"), (512, "v"), (512, "v")],
-    "11": [(512, "s"), (512, "s"), (512, "v"), (512, "v")],
-    "20": [(512, "s"), (512, "s"), (512, "v"), (512, "v")],
-    "21": [(512, "s"), (512, "v"), (512, "v"), (512, "v")],
-}
-PERIOD = 400
-ORDER = {
-    'out':[401,456,517,479,457],'wL':[253,257,259,262,264,402,431,267,268,269,432,478],'i11':[3,18,19,20,21],'x0':[250,404],'f10':[5,6,8,10],
-    'c1':[-288,-273,-213,-100,-102,-354,-324,-232,-164,-160,-124,-372,-353,-351,-350,-252,-184,-249,-323,-205,-162,-173,-111,-174,-204,-348,-112,-103,-274,-270,-189,-106,-286,-285,-266,-221,-219,-224,-222,-300,-223,-218,-235,-163,-220,-278,-209,-271,-269,-254,-253,40,-212,25,11,-199,26,9,7,24,-117],
-    'o0':[-104,12],'d10':[13,14,15,17],'c0':[-308,-309,-558,-347,-287,-384,-330,-339,-306,-293,-296,-284,-251,-272,-200,-245,-190],'o1':[22],'c2':[23,44],
-    's10':[27,37,41,39,42,58,43,60,65,59,62,66,67,80,85,68,86,81,82,96,88,102,103,106,89,90,93],'a10':[29,30,33,34],'wr1':[35,36],'st1':[438],
-    'f11':[55,54,48,45,72,51],'pp0':[63,84,101,97,105,172,110,202,212,154],'a11':[71,74,64,75,95,73],'d11':[87,69],
-    's11':[83,98,99,109,132,133,135,136,138,137,140,142,141,150,153,144,157,156,159,161,174,171,173,175,186,190,194],'f20':[123,108,121,111,118,125],
-    'r0':[119,169,193,204,206,208,217,234,243,249,213,247],'sw0':[120,124],'d20':[139,158],'a20':[145,166,143,164,163,167],
-    'pp1':[152,160,185,183,184,170,189,192,215,246],'sw1':[162,197],'f21':[228,225,199,198,224],'w0':[203,205,209,214,219,223,232,218,220,222,244,245],
-    'd21':[221,207,229],'a21':[231,239,233,230,241],'r1':[235,251,252,254,255,260,263,266,275,278,265,272],'st0':[248],
-    'w1':[256,258,261,270,273,281,290,271,274,279,291,301],'i10':[-123,-120,-113,-114,-107],'cnt':[282,292,295],'wr0':[-116,-101],'x1':[285]}
+BIG = 8192.0
+PLAN = {"10": "p a a a", "11": "a a s s", "20": "a a s s", "21": "v v v s"}
+PIECE = {"10": 512, "11": 512, "20": 512, "21": 512}
+MASK = "table"
+TWO = 1
+RUNS = {"10": (0, 4), "11": (0, 4), "20": (0, 4), "21": (0, 3, 4)}
+GAP = {"10": 4000.0, "11": 0.0, "20": 1000.0, "21": 2000.0, "end": 7000.0}
+LOOK, TRIES, EASE = 150.0, 45000, 150.0
 
 SCRATCH = {
-    "X": ("sbuf", [128, 4128], "bfloat16"),
-    "ST": ("sbuf", [128, 1152], "float32"),
+    "X": ("sbuf", [128, 4144], "bfloat16"),
+    "XL": ("sbuf", [128, 4096], "bfloat16"),
+    "ST": ("sbuf", [128, 3072], "float32"),
     "wdi": ("sbuf", [128, 256], "int32"),
     "pdi": ("sbuf", [128, 1024], "int32"),
     "wti": ("sbuf", [128, 8], "int32"),
-    "wtf": ("sbuf", [128, 8], "float32"),
-    "Ac": ("sbuf", [128, 8], "float32"),
-    "Aq": ("sbuf", [128, 8], "int32"),
+    "col": ("sbuf", [128, 16], "float32"),
+    "Q": ("sbuf", [128, 16], "bfloat16"),
     "val": ("sbuf", [128, 128], "float32"),
     "gv": ("sbuf", [128, 256], "float32"),
-    "CW": ("sbuf", [128, 11 * 128], W16),
-    "Ib": ("sbuf", [128, 512], "bfloat16"),
-    "If": ("sbuf", [128, 256], "float32"),
-    "G8": ("sbuf", [128, 32], "float32"),
-    "RK": ("sbuf", [128, 40], "bfloat16"),
-    "DGi": ("sbuf", [128, 128], "int32"),
-    "DG": ("sbuf", [128, 256], "bfloat16"),
-    "IM": ("sbuf", [128, 128], "int32"),
-    "Li": ("sbuf", [128, 32], "int32"),
-    "L": ("sbuf", [128, 32], "uint16"),
-    "STEP": ("sbuf", [128, 128], "float32"),
-    "rowf": ("sbuf", [128, 128], "float32"),
-    "row": ("sbuf", [128, 1024], "bfloat16"),
+    "CW": ("sbuf", [128, 12 * 128], W16),
+    "Ib": ("sbuf", [128, 7 * 128], "bfloat16"),
+    "RK": ("sbuf", [128, 56], "bfloat16"),
+    "Ci": ("sbuf", [128, 320], "int32"),
+    "DZ": ("sbuf", [128, 112], "bfloat16"),
+    "TJ": ("sbuf", [128, 2048], "bfloat16"),
+    "TP": ("sbuf", [128, 192], "bfloat16"),
+    "EL": ("sbuf", [128, 16], "uint16"),
+    "STEP": ("sbuf", [128, 392], "float32"),
+    "rowf": ("sbuf", [128, 136], "float32"),
+    "row": ("sbuf", [128, 1296], "bfloat16"),
 }
 for _h in range(2):
     for _n, _c, _d in (
         ("F", 2048, "bfloat16"), ("D", 2048, "bfloat16"), ("AD", 2048, "bfloat16"),
-        ("O1", 256, "uint16"), ("O2", 256, "uint16"), ("OS", 40, "uint16"),
-        ("I1", 256, "int32"), ("I2", 256, "int32"), ("P1", 128, "float32"), ("P2", 256, "float32"),
-        ("Wr", 384, "float32"), ("MK", 384, W16), ("B", 128, W16), ("OH", 128, "bfloat16"),
-        ("S1", 384, "float32"), ("S2", 256, "float32"), ("NF", 128, "float32"), ("XD", 384, "float32"),
-        ("XM", 128, "float32"), ("SW", 384, "float32"), ("TP", 32, "int32"), ("CI", 104, "int32"),
-        ("AB", 40, "int32"), ("C3", 24, "int32"), ("NG", 24, "float32"), ("G1", 128, "float32"), ("RI", 128, "int32"),
+        ("O1", 256, "uint16"), ("O2", 256, "uint16"), ("OS", 48, "uint16"),
+        ("I", 256, "int32"), ("P", 256, "float32"),
+        ("MK", 384, W16), ("B", 128, "float32"), ("OH", 128, "bfloat16"), ("MB", 128, W16),
+        ("S1", 408, "float32"), ("S2", 256, "float32"), ("TF", 32, "float32"), ("NF", 136, "float32"), ("SW", 512, "float32"),
+        ("TI", 128, "int32"), ("TB", 32, "bfloat16"), ("XE", 320, W16), ("XB", 64, "bfloat16"), ("BASE", 24, W16),
+        ("G1", 128, "float32"), ("RI", 128, "int32"),
         ("Wl", NV * 128, W16), ("Wo", NV * 128, W16), ("Yl", 128, "float32"), ("Yo", 128, "float32"),
     ):
         SCRATCH["%s%d" % (_n, _h)] = ("sbuf", [128, _c], _d)
     for _b in range(4):
         SCRATCH["b%d%d" % (_b, _h)] = ("psum", [128, 512], "float32")
-SEMAPHORES = ["v", "s", "t", "g", "sent"] + ["d%d" % i for i in range(10)] + ["arr%d" % i for i in range(2 * NV)]
+SEMAPHORES = ["v", "s", "t", "g", "sent"] + ["d%d" % i for i in range(20)] + ["arr%d" % i for i in range(2 * NV)]
 
-CYC, FIX, HOP, PEC, GAT, SCA, DMA, FAR = 1.0, 60.0, 90.0, 0.55, 1.56, 3.8, 2200.0, 3200.0
+FIX, IND, HOP, DMA, BYTE = 60.0, {"v": 50.0, "s": 65.0}, 150.0, 1200.0, 0.33
+FIGURES = [dict(cycle=0.92, gather=1.20, scatter=3.0, pair=1.22, tensor=0.50, v=15.0, s=25.0, t=45.0, psum=45.0, same=155.0, cross=140.0, far=2400.0),
+           dict(cycle=0.84, gather=1.07, scatter=2.4, pair=1.25, tensor=0.46, v=10.0, s=20.0, t=55.0, psum=12.0, same=170.0, cross=195.0, far=1900.0),
+           dict(cycle=1.15, gather=1.55, scatter=4.2, pair=1.15, tensor=0.50, v=60.0, s=95.0, t=80.0, psum=50.0, same=60.0, cross=170.0, far=2400.0)]
 
 
-def v(name, lo, hi, st=1, p=128):
-    return (name, lo, hi, st, p)
+def v(name, lo, hi, st=1, p=128, p0=0):
+    return (name, lo, hi, st, p, p0)
+
+
+def part(x, p0, p):
+    return (x[0], x[1], x[2], x[3], p, p0)
 
 
 def width(x):
     return (x[2] - x[1] + x[3] - 1) // x[3]
 
 
-def build(g, T, nxt):
+def build(g, T, nxt, figures=None):
+    f = figures or FIGURES[0]
+    CYC, GAT, SCA, PEC, FAR = f["cycle"], f["gather"], f["scatter"], f["tensor"], f["far"]
     ops = []
-    now = [(0, "c0")]
+    now = [0, "const", 0]
 
-    def at(t, key):
-        now[0] = (t, key)
+    def at(stage):
+        now[1] = stage
 
     def ap(x):
-        return T[x[0]][0:x[4], x[1]:x[2]:x[3]] if x[3] > 1 else T[x[0]][0:x[4], x[1]:x[2]]
+        return T[x[0]][x[5]:x[4], x[1]:x[2]:x[3]] if x[3] > 1 else T[x[0]][x[5]:x[4], x[1]:x[2]]
 
     def ind(win, off):
         return ap(win).indirect(ap(off))
 
     def add(q, fn, rd, wr, t, kind=None):
-        ops.append((q, fn, [r for r in rd if isinstance(r, tuple)], wr, t, kind, now[0]))
+        rd = [r for r in rd if isinstance(r, tuple)]
+        if isinstance(t, tuple):
+            t = t[0] + (IND[q] if t[1] else f[q]) + (f["psum"] if any(SCRATCH[r[0]][0] == "psum" for r in rd + wr) else 0.0)
+        ops.append((q, fn, rd, wr, t, kind, now[0], now[1], now[2]))
 
     def sc(x):
         return ap(x) if isinstance(x, tuple) else x
 
     def cost(n, r=1.0):
-        return FIX + CYC * max(50.0, n * r)
+        return (f["cycle"] * max(64.0, n * r), r > 1.0 and r != 2.0)
+
+    def rate(o, a, off):
+        short = all(SCRATCH[x[0]][2] in (W16, "bfloat16", "uint16") for x in (o, a))
+        return GAT if off else 0.5 if short else 1.0
 
     V = g.vector
 
     def tt(o, a, b, op, off=None):
         two = SCRATCH[a[0]][0] != "psum" and SCRATCH[b[0]][0] != "psum"
         add("v", lambda: V.tensor_tensor(ap(o), ind(a, off) if off else ap(a), ap(b), op), [a, b, off], [o],
-            cost(width(o), GAT if off else 2.0 if two else 1.0))
+            cost(width(o), GAT * f["pair"] if off else 2.0 if two else 1.0))
 
     def ts(o, a, s1, s2, op0, op1=None, off=None):
         def fn():
@@ -108,10 +114,13 @@ def build(g, T, nxt):
             if op1 is None:
                 return V.tensor_scalar(ap(o), x, sc(s1), None, op0)
             return V.tensor_scalar(ap(o), x, sc(s1), sc(s2), op0, op1)
-        add("v", fn, [a, s1, s2, off], [o], cost(width(o), GAT if off else 1.0))
+        add("v", fn, [a, s1, s2, off], [o], cost(width(o), rate(o, a, off)))
 
     def cp(o, a, off=None):
-        add("v", lambda: V.tensor_copy(ap(o), ind(a, off) if off else ap(a)), [a, off], [o], cost(width(o), GAT if off else 1.0))
+        add("v", lambda: V.tensor_copy(ap(o), ind(a, off) if off else ap(a)), [a, off], [o], cost(width(o), rate(o, a, off)))
+
+    def fill(o, c):
+        add("v", lambda: V.memset(ap(o), c), [], [o], cost(width(o)))
 
     def scan(o, d0, d1, op0, op1):
         add("v", lambda: V.tensor_tensor_scan(ap(o), ap(d0), ap(d1), 0.0, op0, op1), [d0, d1], [o], cost(width(o)))
@@ -126,29 +135,39 @@ def build(g, T, nxt):
             for o, l, r, s0, s1 in group:
                 last = g.tensor.matmul(ap(o), ap(l), ap(r), s0, s1)
             return last
-        t = sum(15.0 + PEC * max(min(64, width(l)), width(r)) * (4 if SCRATCH[l[0]][2] == "float32" else 1) for o, l, r, s0, s1 in group)
-        add("t", fn, [x[1] for x in group] + [x[2] for x in group], [x[0] for x in group], 60.0 + t)
+        t = sum(PEC * max(min(64, width(l)), width(r)) * (4 if SCRATCH[l[0]][2] == "float32" else 1) for o, l, r, s0, s1 in group)
+        add("t", fn, [x[1] for x in group] + [x[2] for x in group], [x[0] for x in group], f["t"] + t)
+
+    def acc(terms):
+        return [(o, l, r, n == 0, n == len(terms) - 1) for n, (o, l, r) in enumerate(terms)]
 
     def iota(o, pat, base, cm):
         flt = SCRATCH[o[0]][2] != "int32"
         add("g", (lambda: g.iota(ap(o), pat, base, cm, allow_small_or_imprecise_dtypes=True)) if flt else (lambda: g.iota(ap(o), pat, base, cm)),
             [], [o], 130.0 + 2 * CYC * width(o))
 
-    def dma(q, o, a, rd, wr, t, **kw):
+    def dma(q, o, a, rd, wr, row, **kw):
         eng = {"y": g.sync, "s": g.scalar, "g": g}[q]
-        add(q, lambda: eng.dma_start(o, a, **kw), rd, wr, t, "dma")
+        add(q, lambda: eng.dma_start(o, a, **kw), rd, wr, DMA + BYTE * row, "dma")
 
-    I16, NI16, SM, SP, NL, NR, LF, LG, GG, G3232, G2080 = [v("CW", 128 * i, 128 * i + 128) for i in range(11)]
-    IB, IBN, IBM, IB2 = [v("Ib", 128 * i, 128 * i + 128) for i in range(4)]
-    IF, ONES = v("If", 0, 128), v("If", 128, 256)
-    ONE, M16, ROW1, ROW2, ROW3 = v("row", 0, 128, 1, 1), v("row", 128, 256, 1, 1), v("row", 256, 512, 1, 1), v("row", 512, 768, 1, 1), v("row", 768, 1024, 1, 1)
-    L15, LB, STEP, Ac = v("L", 0, 16), v("L", 16, 24), v("STEP", 0, 128), v("Ac", 0, 1)
+    I16, SM, SP, NL, NR, LF, LG, GG, G3232, G2080, NLM, NRM = [v("CW", 128 * i, 128 * i + 128) for i in range(12)]
+    IB, IBM, IB2, IBIG, IBIGM, ONES = [v("Ib", 128 * i, 128 * i + 128) for i in range(6)]
+    ZERO = v("Ib", 768, 896)
+    ONE, ROW0, ROW1, ROW1B, ROW2, ROW3, ROW4, ROW5 = [v("row", lo, hi, 1, 1) for lo, hi in (
+        (0, 128), (128, 264), (264, 536), (536, 672), (672, 800), (800, 1056), (1056, 1184), (1184, 1185))]
+    UP, DOWN, FLAT = v("STEP", 0, 128), v("STEP", 128, 263), v("STEP", 264, 392)
+    WT, TAU, Ac = v("col", 0, 1), v("col", 4, 5), v("col", 8, 9)
+    EL2, EL1 = v("EL", 0, 8), v("EL", 8, 12)
+    KEY1, NBR, KEY2, KEY2N, KEY1N, NBRN, WGT = [v("RK", 8 * j, 8 * j + 8) for j in range(7)]
 
-    dma("y", T.wdi[:], T.wd[:], [], [v("wdi", 0, 256)], DMA)
-    dma("y", T.X[:, 0:2048], T.xt[:, 0:2048], [], [v("X", 0, 2048)], DMA + 3500)
-    dma("s", T.X[:, 2048:4096], T.xt[:, 2048:4096], [], [v("X", 2048, 4096)], DMA + 3500)
-    dma("g", T.wti[:, 0:1], T.wt[:], [], [v("wti", 0, 1)], DMA + 1500, allow_slow_non_contiguous=True)
-    dma("y", T.pdi[:], T.pd[:], [], [v("pdi", 0, 1024)], DMA + 5000)
+    def diag(j, e):
+        return v("DZ", 32 * j + 16 - 16 * e, 32 * j + 48 - 16 * e)
+
+    dma("y", T.wdi[:], T.wd[:], [], [v("wdi", 0, 256)], 1024)
+    dma("y", T.X[:, 0:2048], T.xt[:, 0:2048], [], [v("X", 0, 2048)], 8192)
+    dma("s", T.X[:, 2048:4096], T.xt[:, 2048:4096], [], [v("X", 2048, 4096)], 8192)
+    dma("g", T.wti[:, 0:1], T.wt[:], [], [v("wti", 0, 1)], 3000, allow_slow_non_contiguous=True)
+    dma("y", T.pdi[:], T.pd[:], [v("X", 0, 4096)], [v("pdi", 0, 1024)], 4096)
 
     val, gv, gm = v("val", 0, 128), v("gv", 0, 128), v("gv", 128, 256)
     iota(val, [[-1, 128]], 0, 1)
@@ -163,16 +182,17 @@ def build(g, T, nxt):
     tt(LG, NL, NR, A.add)
     for h in range(2):
         ts(v("Wl%d" % h, 0, 128), v("wdi", 128 * h, 128 * h + 128), -2048.0, None, A.add)
-    at(0, "c1")
-    ts(NI16, val, 0.0, -1.0, A.is_equal, A.mult)
     ts(SM, val, -1.0, None, A.is_equal)
     ts(v("CW", SM[1], SM[2], 16), v("val", 0, 128, 16), 15.0, None, A.is_equal)
-    tt(NL, I16, SP, A.subtract)
-    tt(NR, I16, SM, A.subtract)
-    act(IF, val, F.Abs)
-    act(IF, IF, F.Relu, bias=1.0, scale=-1.0)
-    for o, c in ((IB, 1.0), (IBN, -2048.0), (IBM, -1.0), (IB2, 2.0)):
-        act(o, IF, F.Identity, scale=c)
+    tt(NL, SP, I16, A.subtract)
+    tt(NR, SM, I16, A.subtract)
+    if MASK != "table":
+        ts(NLM, NL, -1.0, None, A.mult)
+        ts(NRM, NR, -1.0, None, A.mult)
+    iota(ZERO, [[0, 128]], 0, 0)
+    for o, c in ((IB, 1.0), (IBM, -1.0), (IB2, 2.0), (IBIG, BIG), (IBIGM, -BIG)):
+        add("g", lambda o=o, c=c: g.affine_select(ap(o), ap(ZERO), [[-1, 128]], A.not_equal, c, 0, 1), [ZERO], [o], 170.0 + 256 * CYC)
+    iota(ONES, [[0, 128]], 1, 0)
     iota(gv, [[-32, 8], [0, 16]], -15, 2)
     act(gv, gv, F.Abs)
     act(gm, gv, F.Sign, bias=16.0, scale=-1.0)
@@ -181,214 +201,287 @@ def build(g, T, nxt):
     ts(G3232, gm, 3232.0, None, A.mult)
     ts(G2080, gm, 2080.0, None, A.mult)
     g8 = v("gv", 128, 256, 16)
-    for j in range(4):
-        act(v("G8", 8 * j, 8 * j + 8), g8, F.Identity, scale=1.0 if j < 2 else -1.0)
-    cp(v("wtf", 0, 1), v("wti", 0, 1))
-    for j, c in enumerate((16.0, -1.0, 1.0, -2048.0, v("wtf", 0, 1))):
-        act(v("RK", 8 * j, 8 * j + 8), g8, F.Identity, scale=c)
-    iota(v("DGi", 0, 128), [[0, 8], [-1, 16]], 16, 1)
-    ts(v("DGi", 0, 128), v("DGi", 0, 128), 15, None, A.bitwise_and)
-    ts(v("DG", 0, 128), v("DGi", 0, 128), 0.0, None, A.is_equal)
-    act(v("DG", 128, 256), v("DG", 0, 128), F.Copy)
-    iota(v("Li", 0, 16), [[16, 16]], 15, 0)
-    iota(v("Li", 16, 24), [[1, 8]], 0, 0)
-    cp(v("L", 0, 24), v("Li", 0, 24))
-    iota(STEP, [[0, 128]], 1, 0)
-    iota(v("STEP", 0, 128, 16), [[0, 8]], -16000000, 0)
-    iota(v("IM", 0, 128), [[0, 8], [1, 16]], 0, 0)
-    iota(ONES, [[0, 128]], 1, 0)
-    r15 = v("rowf", 0, 128, 1, 1)
-    iota(r15, [[0, 8], [-1, 16]], 15, 0)
+    cp(WT, v("wti", 0, 1))
+    for o, c in ((KEY1, -2048.0), (KEY1N, 2048.0), (NBR, 2.0 ** -12), (NBRN, -2.0 ** -12), (KEY2, -4096.0), (KEY2N, 4096.0), (WGT, WT)):
+        act(o, g8, F.Identity, scale=c)
+    iota(v("Ci", 128, 256), [[0, 8], [-1, 16]], 16, 1)
+    iota(v("Ci", 256, 320), [[1, 16], [1, 4]], 15, 1)
+    ts(v("Ci", 128, 320), v("Ci", 128, 320), 15, None, A.bitwise_and)
+    ts(v("TJ", 0, 128), v("Ci", 128, 256), 0.0, None, A.is_equal)
+    for j, c in enumerate((0.0, 15.0, 1.0)):
+        ts(v("TP", 64 * j, 64 * j + 64), v("Ci", 256, 320), c, None, A.is_equal)
+    iota(v("DZ", 0, 112), [[0, 112]], 0, 0)
+    for j, c in enumerate((1.0, 1024.0, 128.0)):
+        act(v("DZ", 32 * j + 16, 32 * j + 32), v("TJ", 0, 16), F.Identity, scale=c)
+    for n in (128, 256, 512, 1024):
+        dma("y", T.TJ[:, n:2 * n], T.TJ[:, 0:n], [v("TJ", 0, n)], [v("TJ", n, 2 * n)], 2 * n)
+    P_, C0, CC, R8, X2, X1 = v("Ci", 80, 81), v("Ci", 81, 82), v("Ci", 82, 83), v("Ci", 83, 84), v("Ci", 88, 96), v("Ci", 96, 100)
+    iota(P_, [[0, 1]], 0, 1)
+    ts(C0, P_, 4, None, A.arith_shift_right)
+    ts(CC, P_, 7, None, A.bitwise_and)
+    ts(R8, P_, 8, None, A.bitwise_and)
+    tt(v("col", 1, 2), C0, CC, A.is_equal)
+    cp(v("col", 2, 3), R8)
+    ts(v("col", 3, 4), R8, 0.125, None, A.mult)
+    iota(X2, [[1, 8]], -24, 0)
+    iota(X1, [[2, 4]], -24, 0)
+    ts(X2, X2, v("col", 2, 3), v("col", 1, 2), A.add, A.mult)
+    ts(X1, X1, v("col", 3, 4), v("col", 1, 2), A.add, A.mult)
+    ts(v("EL", 0, 12), v("Ci", 88, 100), 24.0, None, A.add)
+    iota(TAU, [[0, 1]], 15 if TWO else -17, 16)
+    for h in range(2 * TWO):
+        iota(v("TF%d" % h, 0, 32), [[0, 32]], -15, -16)
+    iota(UP, [[0, 128]], 1, 0)
+    iota(v("STEP", 0, 128, 16), [[0, 8]], 1 - 2 ** 24, 0)
+    if TWO:
+        ts(FLAT, UP, -1.0, None, A.add)
+    iota(DOWN, [[0, 135]], -1, 0)
+    iota(v("STEP", 128, 263, 17), [[0, 8]], 2 ** 24 - 1, 0)
+    r15 = v("rowf", 0, 136, 1, 1)
+    iota(r15, [[0, 8], [-1, 17]], 15, 0)
     iota(ONE, [[0, 128]], 1, 0)
-    iota(M16, [[-16, 128]], 0, 0)
-    act(v("row", 256, 384, 1, 1), r15, F.Identity, bias=4096.0, scale=8192.0)
-    act(v("row", 384, 512, 1, 1), r15, F.Identity, scale=1048576.0)
-    iota(v("row", 512, 640, 1, 1), [[0, 128]], 0, 0)
-    act(v("row", 640, 768, 1, 1), r15, F.Identity, bias=2048.0, scale=4096.0)
+    act(ROW0, r15, F.Relu, scale=1048576.0)
+    act(v("row", 264, 400, 1, 1), r15, F.Identity, scale=0.0)
+    act(v("row", 400, 536, 1, 1), r15, F.Relu, bias=1.5, scale=4.0)
+    act(ROW1B, r15, F.Identity, bias=2.0 ** -13, scale=0.0)
+    iota(ROW2, [[0, 128]], -32, 0)
     iota(ROW3, [[1152, 2], [0, 128]], 2080, 0)
-    TI = v("CI0", 0, 8)
-    iota(TI, [[0, 8]], 0, 1)
-    ts(TI, TI, 15, None, A.bitwise_and)
-    iota(v("CI0", 8, 16), [[16, 8]], 0, 0)
-    tt(TI, TI, v("CI0", 8, 16), A.add)
+    iota(ROW4, [[0, 128]], -int(BIG), 0)
+    iota(ROW5, [[0, 1]], 5120, 0)
+    TL = v("Ci", 104, 112)
+    iota(TL, [[0, 8]], 0, 1)
+    ts(TL, TL, 15, None, A.bitwise_and)
+    iota(v("Ci", 112, 120), [[16, 8]], 0, 0)
+    tt(TL, TL, v("Ci", 112, 120), A.add)
     for h in range(2):
-        cp(v("AB%d" % h, 0, 8), TI)
-        ts(v("AB%d" % h, 32, 40), TI, 1024.0, None, A.add)
-        ts(v("C3%d" % h, 0, 8), TI, 4.0, 512.0 * h, A.mult, A.add)
-        ts(v("C3%d" % h, 8, 16), TI, 16.0, None, A.mult)
-        ts(v("C3%d" % h, 16, 24), TI, 128.0, None, A.add)
-    at(0, "c2")
+        ts(v("BASE%d" % h, 0, 8), TL, 16.0, None, A.mult)
+        ts(v("BASE%d" % h, 8, 16), TL, 4.0, 512.0 * h, A.mult, A.add)
+        cp(v("BASE%d" % h, 16, 24), TL)
+        iota(v("TI%d" % h, 0, 128), [[0, 128]], 0, 0)
+        iota(v("TB%d" % h, 0, 32), [[0, 32]], 0, 0)
     cp(v("ST", 0, 1024), v("pdi", 0, 1024))
-    iota(v("ST", 1024, 1152), [[0, 128]], 0, 0)
+    for n in (1024, 2048):
+        dma("y", T.ST[:, n:n + 1024], T.ST[:, 0:1024], [v("ST", 0, 1024)], [v("ST", n, n + 1024)], 4096)
 
     def names(h):
         return lambda n, lo, hi, st=1: v("%s%d" % (n, h), lo, hi, st)
 
     def numbers(o, i, t):
         if t:
-            ts(o, i, Ac, None, A.add)
+            ts(o, i, Ac, None, A.subtract)
         else:
             cp(o, i)
 
     def gathers(t, h, step):
         u = names(h)
         Xw = v("X", 0, 4128 if t else 4096)
-        key = "%d%d" % (step, h)
-        off, lo, n = "O%d" % step, 0, 0
-        for size, who in PLAN[key]:
-            hi = lo + size
+        off, n = "O%d" % step, 0
+        hi = 0
+        for piece in PLAN["%d%d" % (step, h)].split():
+            who, lo, hi = piece[0], hi, hi + 512 * len(piece)
             o1, o2 = u(off, lo // 16, hi // 16), u(off, 128 + lo // 16, 128 + hi // 16)
-            at(t, "f" + key)
-            if who == "s":
+            at("get%d" % step)
+            if who in "sp":
                 act(u("F", lo, hi), Xw, F.Identity, off=o1, scale=1.0 / step)
-                act(u("D", lo, hi), Xw, F.Copy, off=o2)
-                at(t, "a" + key)
+                if who == "s":
+                    act(u("D", lo, hi), Xw, F.Copy, off=o2)
+                else:
+                    cp(u("D", lo, hi), Xw, off=o2)
+                at("abs%d" % step)
                 for s in range(lo, hi, 512):
-                    e = min(hi, s + 512)
-                    bank = u("b3" if n % 2 == 0 else "b1", 0, e - s)
+                    bank = u("b3" if n % 2 == 0 else "b0", 0, 512)
                     n += 1
-                    mm([(bank, IB if step == 1 else IB2, u("F", s, e), True, False), (bank, IBM, u("D", s, e), False, True)])
-                    act(u("AD", s, e), bank, F.Abs)
+                    mm(acc([(bank, IB if step == 1 else IB2, u("F", s, s + 512)), (bank, IBM, u("D", s, s + 512))]))
+                    act(u("AD", s, s + 512), bank, F.Abs)
             else:
                 act(u("F", lo, hi), Xw, F.Copy, off=o1)
-                at(t, "d" + key)
-                tt(u("D", lo, hi), Xw, u("F", lo, hi), A.subtract, off=o2)
-                at(t, "a" + key)
-                act(u("AD", lo, hi), u("D", lo, hi), F.Abs)
-            lo = hi
+                w = PIECE["%d%d" % (step, h)]
+                for s in range(lo, hi, w):
+                    tt(u("D", s, s + w), Xw, u("F", s, s + w), A.subtract, off=u(off, 128 + s // 16, 128 + (s + w) // 16))
+                at("abs%d" % step)
+                if who == "a":
+                    act(u("AD", lo, hi), u("D", lo, hi), F.Abs)
+                else:
+                    ts(u("AD", lo, hi), u("D", lo, hi), 0.0, 2.0, A.max, A.mult)
+
+    def runs(h, step):
+        key = "%d%d" % (step, h)
+        u = names(h)
+        for a, b in zip(RUNS[key], RUNS[key][1:]):
+            lo, hi = 512 * a, 512 * b
+            form = set(c == "v" for c in PLAN[key].replace(" ", "")[a:b])
+            assert len(form) == 1
+            dist = [[u(n, lo + k, hi, 16) for k in range(16)] for n in (("D", "AD") if True in form else ("AD",))]
+            yield 32 * a, 32 * b, dist, [u("F", lo + k, hi, 16) for k in range(16)]
+
+    def spread(terms, base=None):
+        out = []
+        for a in range(4):
+            first = [(part(base[0], 32 * a, 32 * a + 32), v("CW", 32 * a, 32 * a + 32), base[1])] if base else []
+            out += acc(first + [(part(o, 32 * a, 32 * a + 32), diag(j, e), v(x[0], x[1] + n * (2 * a + e), x[1] + n * (2 * a + e + 1)))
+                                for o, x, n, j in terms for e in range(2)])
+        return out
 
     def step1(t, h):
         u = names(h)
         W = u("Wl", 128 * t, 128 * t + 128)
-        at(t, "i1%d" % h)
-        mm([(u("b1", 256, 384), SP, W, True, True), (u("b2", 0, 128), LF, W, True, True), (u("b2", 128, 256), LG, W, True, True)])
-        tt(u("P1", 0, 128), u("b1", 256, 384), W, A.mult)
-        tt(u("I1", 0, 128), u("b2", 0, 128), u("P1", 0, 128), A.add)
-        tt(u("I1", 128, 256), u("b2", 128, 256), u("P1", 0, 128), A.add)
-        ts(u("I1", 0, 256), u("I1", 0, 256), 5, 4095, A.arith_shift_right, A.bitwise_and)
-        at(t, "o%d" % h)
-        for lo, hi in ((0, 128), (128, 256)) if h == 0 else ((0, 256),):
-            numbers(u("O1", lo, hi), u("I1", lo, hi), t)
-        at(t, "wr%d" % h)
-        mm([(u("b1", 0, 128), SM, W, True, True), (u("b1", 128, 256), NI16, W, True, True)])
-        act(u("Wr", 0, 384), u("b1", 0, 384), F.Copy)
+        at("addr1")
+        mm([(u("b0", 0, 128), SP, W, True, True), (u("b0", 128, 256), LF, W, True, True), (u("b0", 256, 384), LG, W, True, True)])
+        tt(u("P", 0, 128), u("b0", 0, 128), W, A.mult)
+        tt(u("I", 0, 128), u("b0", 128, 256), u("P", 0, 128), A.add)
+        tt(u("I", 128, 256), u("b0", 256, 384), u("P", 0, 128), A.add)
+        for lo, hi in ((0, 128), (128, 256)) if h else ((0, 256),):
+            ts(u("I", lo, hi), u("I", lo, hi), 5, 4095, A.arith_shift_right, A.bitwise_and)
+        for lo, hi in ((0, 128), (128, 256)):
+            numbers(u("O1", lo, hi), u("I", lo, hi), t)
         gathers(t, h, 1)
-        at(t, "s1%d" % h)
-        mm([(u("b2", 0, 256), ONE, ROW1, True, False)] +
-           [(u("b2", 128 + k, 256, 16), u("F", k, 2048, 16), v("RK", 32, 40), False, False) for k in range(16)])
-        a = [u("AD", k, 2048, 16) for k in range(16)]
-        mm([(u("b0", k, 128, 16), a[k], v("RK", 0, 8), True, True) for k in range(16)])
-        mm([(u("b2", (k + d) % 16, 128, 16), a[k], v("RK", 12 + 4 * d, 20 + 4 * d), False, k == 15 and d == 1) for k in range(16) for d in (-1, 1)])
-        scan(u("S1", 256, 384), STEP, u("b0", 0, 128), A.add, A.max)
-        tt(u("NF", 0, 128), u("b0", 0, 128), u("S1", 256, 384), A.not_equal)
-        scan(u("S1", 0, 128), u("NF", 0, 128), u("b2", 128, 256), A.mult, A.max)
-        scan(u("S1", 128, 256), u("NF", 0, 128), u("b2", 0, 128), A.mult, A.max)
-        tt(u("XD", 0, 128), u("S1", 0, 128), v("DG", 0, 128), A.mult, off=v("L", 0, 8))
-        mm([(u("b0", 384, 392), u("XD", 0, 128), v("G8", 0, 8), True, True)])
-        ts(u("TP", 0, 8), u("S1", 128 + 15, 256, 16), -1.0 / 8192, 16.0 - 2.0 ** -14, A.mult, A.add)
-        ts(u("TP", 8, 16), u("TP", 0, 8), 15, None, A.bitwise_and)
-        tt(u("OH", 0, 128), u("TP", 8, 16), v("IM", 0, 128), A.is_equal, off=LB)
-        cp(u("CI", 0, 8), u("b0", 384, 392))
-        ts(u("CI", 16, 24), u("CI", 0, 8), 1023, None, A.bitwise_and)
-        cp(u("OS", 0, 8), u("CI", 16, 24))
-        mm([(u("b2", 128 * j, 128 * j + 128), u("OH", 0, 128), IB, True, True) for j in range(3)])
-        ts(u("B", 0, 128), v("ST", 0, 1024), -2048.0, None, A.add, off=u("OS", 0, 8))
-        tt(u("MK", 0, 384), u("b2", 0, 384), u("Wr", 0, 384), A.mult)
+        for p0, p1, dist, first in runs(h, 1):
+            def out(bank, lo, hi, st=1):
+                return part(u(bank, lo, hi, st), p0, p1)
+            one = v("row", 0, p1 - p0, 1, 1)
+            at("u")
+            mm(acc([(out("b2", 0, 136), one, ROW0)] + [(out("b2", k, 136, 17), first[k], WGT) for k in range(16)]))
+            at("key1")
+            terms = [(out("b1", 0, 272), one, ROW1), (out("b1", 136, 272), one, ROW1B)]
+            for s, d in enumerate(dist):
+                w = 32 * (s < len(dist) - 1)
+                terms += [(out("b1", k + 1, 272, 17), d[k], v("RK", w, w + 16)) for k in range(15)]
+                terms += [(out("b1", 16, 136, 17), d[15], v("RK", w, w + 8)), (out("b1", 136, 272, 17), d[15], v("RK", w + 8, w + 16))]
+                terms += [(out("b1", 136 + (k - 1) % 16, 272, 17), d[k], v("RK", 40 - w, 48 - w)) for k in range(16)]
+            terms = acc(terms)
+            mm(terms[:-33])
+            mm(terms[-33:])
+        at("dec1")
+        scan(u("S1", 272, 407), DOWN, u("b1", 1, 136), A.add, A.min)
+        tt(u("NF", 0, 135), u("b1", 1, 136), u("S1", 272, 407), A.not_equal)
+        scan(u("S1", 0, 135), u("NF", 0, 135), u("b2", 0, 135), A.mult, A.max)
+        scan(u("S1", 136, 271), u("NF", 0, 135), u("b1", 136, 271), A.mult, A.max)
+        cp(u("TI", 0, 16), u("S1", 15, 272, 17))
+        ts(u("TI", 32, 48), u("TI", 0, 16), 1023, None, A.bitwise_and)
+        cp(u("XE", 0, 128), u("TI", 32, 64), off=EL2)
+        mm(spread([(u("b1", 288, 304), u("XE", 0, 128), 16, 0)]))
+        cp(u("OS", 0, 16), u("b1", 288, 304))
+        act(u("B", 0, 128), v("ST", 0, 1024), F.Identity, off=u("OS", 0, 8), bias=-2048.0)
 
     def step2(t, h):
         u = names(h)
         W = u("Wl", 128 * t, 128 * t + 128)
-        ma, mp, mb = u("MK", 0, 128), u("MK", 128, 256), u("MK", 256, 384)
-        at(t, "s1%d" % h)
-        mm([(u("b1", 256, 384), G3232, ma, True, True), (u("b1", 384, 512), G2080, mb, True, True),
-            (u("b1", 0, 256), ONE, ROW3, True, False), (u("b1", 0, 128), GG, ma, False, False), (u("b1", 128, 256), GG, mb, False, True)])
-        tt(u("P2", 0, 128), u("b1", 0, 128), u("B", 0, 128), A.mult)
-        tt(u("P2", 128, 256), u("b1", 128, 256), u("B", 0, 128), A.mult)
-        for lo, hi in ((0, 128), (128, 256)):
-            tt(u("I2", lo, hi), u("b1", 256 + lo, 256 + hi), u("P2", lo, hi), A.add)
-            ts(u("I2", lo, hi), u("I2", lo, hi), 5, 4095, A.arith_shift_right, A.bitwise_and)
-            numbers(u("O2", lo, hi), u("I2", lo, hi), t)
-        at(t, "sw%d" % h)
-        mm([(u("b3", 128, 256), I16, W, True, False), (u("b3", 128, 256), NL, ma, False, False), (u("b3", 128, 256), NL, mp, False, True),
-            (u("b3", 256, 384), I16, W, True, False), (u("b3", 256, 384), NR, mb, False, False), (u("b3", 256, 384), NR, mp, False, True)])
-        act(u("SW", 128, 384), u("b3", 128, 384), F.Copy)
-        at(t, "pp%d" % h)
-        tt(u("XD", 128, 384), u("S1", 128, 384), v("DG", 0, 256), A.mult, off=L15)
-        mm([(u("b2", 392, 400), u("XD", 128, 256), v("G8", 0, 8), True, True), (u("b2", 400, 416), u("XD", 256, 384), v("G8", 0, 16), True, True)])
-        cp(u("CI", 8, 16), u("b2", 392, 400))
-        ts(u("CI", 24, 40), u("b2", 400, 416), 1.0 / 32, 1.0 / 64, A.mult, A.add)
-        ts(u("CI", 40, 48), u("CI", 0, 8), 3, None, A.bitwise_and)
-        ts(u("CI", 48, 56), u("CI", 0, 8), 15, None, A.bitwise_and)
-        ts(u("CI", 56, 64), u("CI", 8, 16), 5, 128, A.arith_shift_right, A.bitwise_and)
-        tt(u("AB", 8, 32), u("CI", 40, 64), u("C3", 0, 24), A.add)
-        cp(u("OS", 16, 24), u("AB", 16, 24))
-        ts(u("CI", 24, 40), u("CI", 24, 40), 2048.0, None, A.mult)
+        ma, mb, mp = u("MK", 0, 128), u("MK", 128, 256), u("MK", 256, 384)
+        OH, B = u("OH", 0, 128), u("B", 0, 128)
+        at("addr2")
+        act(OH, v("TP", 0, 64), F.Copy, off=u("OS", 8, 16))
+        if MASK != "table":
+            mm([(u("b2", 136, 264), SM, W, True, True), (u("b2", 264, 392), SP, W, True, True)])
+        for j, (bank, m, lin) in enumerate((("b0", ma, G3232), ("b3", mb, G2080))):
+            lo, hi = 128 * j, 128 * j + 128
+            both = acc([(u(bank, 0, 128), ONE, v("row", ROW3[1] + lo, ROW3[1] + hi, 1, 1)), (u(bank, 0, 128), GG, m)])
+            mm(both[:1])
+            if MASK == "table":
+                tt(m, v("TP", 64 + 64 * j, 128 + 64 * j), W, A.mult, off=u("OS", 8, 16))
+            else:
+                tt(m, u("b2", 136 + lo, 136 + hi), OH, A.mult)
+            mm(both[1:] + [(u(bank, 128, 256), lin, m, True, True)])
+            tt(u("P", lo, hi), u(bank, 0, 128), B, A.mult)
+            tt(u("I", lo, hi), u(bank, 128, 256), u("P", lo, hi), A.add)
+            ts(u("I", lo, hi), u("I", lo, hi), 5, 4095, A.arith_shift_right, A.bitwise_and)
+            numbers(u("O2", lo, hi), u("I", lo, hi), t)
+        at("side")
+        mm([(u("b2", 0, 128), I16, W, True, True)])
+        tt(mp, u("b2", 0, 128), OH, A.mult)
+        if MASK == "table":
+            left, right = [(NR, ma), (NL, mp)], [(NL, mb), (NR, mp)]
+        else:
+            left, right = [(NLM, ma), (NL, mp)], [(NRM, mb), (NR, mp)]
+        mm(acc([(u("b2", 0, 128), l, r) for l, r in [(I16, W)] + left]) + acc([(u("b2", 128, 256), l, r) for l, r in [(I16, W)] + right]) +
+           acc([(u("b2", 256, 384), I16, W), (u("b2", 256, 384), IBIGM, OH)]))
+        act(u("SW", 128, 512), u("b2", 0, 384), F.Copy)
+        ts(u("TI", 64, 72), u("TI", 32, 40), 15, None, A.bitwise_and)
+        ts(u("TI", 72, 88), u("TI", 32, 48), 3, None, A.bitwise_and)
+        cp(u("XE", 128, 256), u("TI", 64, 96), off=EL2)
         gathers(t, h, 2)
-        at(t, "r%d" % h)
-        mm([(u("b0", 0, 256), ONE, ROW2, True, False), (u("b0", 0, 128), M16, ONE, False, False), (u("b0", 128, 256), u("B", 0, 128), I16, False, False)])
-        mm([(u("b0", k, 128, 16), u("AD", k, 2048, 16), v("RK", 24, 32), False, k == 15) for k in range(16)])
-        scan(u("S2", 0, 128), STEP, u("b0", 0, 128), A.add, A.max)
-        tt(u("XD", 0, 128), u("S2", 0, 128), v("DG", 0, 128), A.mult, off=v("L", 0, 8))
-        mm([(u("b2", 416, 432), u("XD", 0, 128), v("G8", 16, 32), True, True)])
-        ts(u("CI", 64, 80), u("b2", 416, 432), 15.0, None, A.add)
-        ts(u("CI", 80, 88), u("CI", 64, 72), 2047, None, A.bitwise_and)
-        cp(u("OS", 8, 16), u("CI", 80, 88))
-        act(u("G1", 0, 128), u("D", 0, 2048), F.Identity, off=u("OS", 8, 16), bias=-0.25, scale=0.5)
-        tt(u("RI", 0, 128), u("F", 0, 2048), u("G1", 0, 128), A.add, off=u("OS", 8, 16))
-        tt(u("NG", 0, 16), u("CI", 64, 80), u("CI", 24, 40), A.is_ge)
+        for p0, p1, dist, first in runs(h, 2):
+            at("key2")
+            key = acc([(part(u("b1", 0, 128), p0, p1), v("row", 0, p1 - p0, 1, 1), ROW2)] +
+                      [(part(u("b1", k, 128, 16), p0, p1), d[k], (KEY2N, KEY2)[s == len(dist) - 1]) for s, d in enumerate(dist) for k in range(16)])
+            mm(key[:17])
+            if len(dist) == 2:
+                mm(key[17:])
+        at("dec2")
+        scan(u("S2", 0, 128), UP, u("b1", 0, 128), A.add, A.max)
+        if TWO:
+            scan(u("S2", 128, 256), FLAT, u("b1", 0, 128), A.add, A.max)
+        last = u("S2", 15, 128, 16)
+        tt(u("TB", 8, 16), last, u("S1", 272 + 15, 407, 17), A.is_lt)
         if t < NV - 1:
-            add("v", lambda: V.tensor_reduce(ap(u("NG", 16, 17)), ap(u("NG", 0, 8)), AX.X, A.add), [u("NG", 0, 8)], [u("NG", 16, 17)], cost(8))
-        at(t, "wL" if t == NV - 1 and h else "w%d" % h)
-        tt(u("NF", 0, 128), u("b0", 0, 128), u("S2", 0, 128), A.not_equal)
-        scan(u("S2", 128, 256), u("NF", 0, 128), u("b0", 128, 256), A.mult, A.max)
-        cp(u("TP", 16, 24), u("S2", 128 + 15, 256, 16))
-        ts(u("TP", 24, 32), u("TP", 16, 24), 4095, None, A.bitwise_and)
-        tt(u("XM", 0, 128), u("TP", 24, 32), u("OH", 0, 128), A.mult, off=LB)
-        mm([(u("b3", 0, 128), I16, W, True, False), (u("b3", 0, 128), I16, mp, False, False),
-            (u("b3", 0, 128), u("OH", 0, 128), IBN, False, False), (u("b3", 0, 128), u("XM", 0, 128), IF, False, True)])
-        act(u("SW", 0, 128), u("b3", 0, 128), F.Copy)
-        tt(u("CI", 88, 104), u("NG", 0, 16), u("AB", 24, 40), A.mult)
-        tt(u("CI", 88, 104), u("CI", 88, 104), u("AB", 0, 16), A.max)
-        cp(u("OS", 24, 40), u("CI", 88, 104))
+            at("count")
+            c = u("b3", 0, 1)
+            mm(acc(([(c, ONE, ROW5)] if h == 0 else []) + [(c, ONES, u("TB", 8 + j, 9 + j)) for j in range(8)]))
+            at("dec2")
+        if TWO:
+            tt(u("TF", 0, 8), u("S2", 128 + 15, 256, 16), last, A.subtract)
+            ts(u("XE", 256, 320), u("TF", 0, 32), TAU, None, A.add, off=EL1)
+        else:
+            ts(u("TI", 16, 24), last, -1.0, TAU, A.mult, A.add)
+            ts(u("TI", 96, 104), u("TI", 16, 24), 4095, None, A.bitwise_and)
+            cp(u("XE", 256, 320), u("TI", 96, 128), off=EL1)
+        mm(spread([(u("b1", 256, 264), u("XE", 256, 320), 8, 0)]))
+        slot = u("OS", 16, 24)
+        cp(slot, u("b1", 256, 264))
+        at("words")
+        tt(u("MB", 0, 128), v("TJ", 0, 2048), B, A.mult, off=slot)
+        mm(acc([(u("b0", 0, 128), ONE, ROW4), (u("b0", 0, 128), IBIG, OH), (u("b0", 0, 128), GG, u("MB", 0, 128))]))
+        tt(u("SW", 0, 128), u("b0", 0, 128), u("SW", 384, 512), A.max)
+        tt(u("TB", 0, 8), u("TB", 8, 16), u("TI", 80, 88), A.mult)
+        act(u("XB", 0, 64), u("TB", 0, 32), F.Copy, off=EL1)
+        mm(spread([(u("b2", 384, 400), u("XE", 128, 256), 16, 0), (u("b2", 392, 400), u("XB", 0, 64), 8, 1),
+                   (u("b2", 400, 408), u("XB", 0, 64), 8, 2)], (u("b2", 384, 408), u("BASE", 0, 24))))
+        cp(u("OS", 24, 48), u("b2", 384, 408))
+        at("rec")
+        act(u("G1", 0, 128), u("D", 0, 2048), F.Identity, off=slot, bias=-0.25, scale=0.5)
+        tt(u("RI", 0, 128), u("F", 0, 2048), u("G1", 0, 128), A.add, off=slot)
+        at("words")
         if t < NV - 1:
             src, dst = u("Wo", 128 * t, 128 * t + 128), u("Wl", 128 * t + 128, 128 * t + 256)
-            cp(src, u("SW", 0, 384), off=u("OS", 24, 32))
+            act(src, u("SW", 0, 384), F.Copy, off=u("OS", 40, 48))
         else:
             src, dst = u("Yo", 0, 128), u("Yl", 0, 128)
-            act(src, u("SW", 0, 384), F.Identity, off=u("OS", 24, 32), bias=2048.0)
+            act(src, u("SW", 0, 384), F.Identity, off=u("OS", 40, 48), bias=2048.0)
         sem = T.sem["arr%d" % (2 * t + h)]
         add("g", lambda: g.remote_dma(ap(dst), ap(src), sem, T.sem.sent, nxt[1], nxt[0], nxt[2]), [src], [dst], FAR, ("far", "arr%d" % (2 * t + h)))
 
     def writes(t, h):
         u = names(h)
-        at(t, "x%d" % h)
-        xw, o = v("X", 2048 * h, 2048 * h + 2048), u("OS", 16, 24)
+        at("put")
+        xw, o = v("X" if t < NV - 1 else "XL", 2048 * h, 2048 * h + 2048), u("OS", 24, 32)
         add("v", lambda: V.tensor_copy(ind(xw, o), ap(u("RI", 0, 128))), [o, u("RI", 0, 128)], [xw], cost(128, SCA))
         if h == 0 and t < NV - 1:
+            at("wrap")
             act(v("X", 4096, 4128), v("X", 0, 32), F.Copy)
-        at(t, "st%d" % h)
-        sw, o2 = v("ST", 0, 1152), u("OS", 32, 40)
+        at("stock")
+        sw, o2 = v("ST", 0, 3072), u("OS", 32, 40)
         add("v", lambda: V.tensor_scalar(ind(sw, o2), ap(u("SW", 0, 128)), 1.0, 2048.0, A.mult, A.add), [o2, u("SW", 0, 128)], [sw], cost(128, SCA))
+        if t == NV - 1:
+            at("out")
+            lo, hi = 2048 * h, 2048 * h + 2048
+            dma("y", T.yx[:, lo:hi], T.XL[:, lo:hi], [v("XL", lo, hi)], [], 4096)
+            dma("s" if h else "y", T.yp[:, 512 * h:512 * h + 512], T.ST[:, 512 * h:512 * h + 512], [v("ST", 512 * h, 512 * h + 512)], [], 2048)
+            dma("y", T.yw[:, 128 * h:128 * h + 128], T["Yl%d" % h][:], [v("Yl%d" % h, 0, 128)], [], 512)
 
     for t in range(NV):
-        step1(t, 0)
-        step1(t, 1)
-        step2(t, 0)
-        step2(t, 1)
-        writes(t, 0)
-        writes(t, 1)
+        now[2] = t
+        if t == NV - 1:
+            at("keep")
+            dma("y", T.XL[:], T.X[:, 0:4096], [v("X", 0, 4096)], [v("XL", 0, 4096)], 8192)
+        for step in (step1, step2, writes):
+            for h in range(2):
+                now[0] = h
+                step(t, h)
         if t < NV - 1:
-            at(t, "cnt")
-            c = v("b21", 432, 433)
-            mm([(c, ONES, v("NG0", 16, 17), True, False), (c, ONES, v("NG1", 16, 17), False, True)])
-            ts(v("Aq", 0, 1), c, 1.0 / 32, -15.5 / 32, A.mult, A.add)
-            ts(Ac, v("Aq", 0, 1), -32.0, c, A.mult, A.add)
-    at(NV - 1, "out")
-    for h in range(2):
-        q = "ys"[h]
-        dma(q, T.yx[:, 2048 * h:2048 * h + 2048], T.X[:, 2048 * h:2048 * h + 2048], [v("X", 2048 * h, 2048 * h + 2048)], [], DMA + 2500)
-        dma("y", T.yw[:, 128 * h:128 * h + 128], T["Yl%d" % h][:], [v("Yl%d" % h, 0, 128)], [], DMA)
-    dma("y", T.yp[:], T.ST[:, 0:1024], [v("ST", 0, 1024)], [], DMA + 2500)
+            at("count")
+            c0, c1, Q = v("b30", 0, 1), v("b31", 0, 1), v("Q", 0, 1)
+            ts(Q, c1, c0, -15.5, A.add, A.add)
+            ts(Ac, Q, c0, c1, A.subtract, A.subtract)
+        now[0] = 0
     return ops
 
 
@@ -401,11 +494,11 @@ def depend(ops):
         for r, w in acc:
             ps = SCRATCH[r[0]][0] == "psum"
             for j, lo, hi, w2 in seen.get(r[0], []):
-                if (ps and ops[j][0] != o[0]) or ((w or w2) and lo < r[2] and r[1] < hi):
+                if (ps and (ops[j][0] != o[0] or o[0] == "t")) or ((w or w2) and lo < r[2] and r[1] < hi):
                     d.add(j)
         for r, w in acc:
             lst = seen.setdefault(r[0], [])
-            if w and r[3] == 1 and r[4] == 128 and SCRATCH[r[0]][0] != "psum":
+            if w and r[3] == 1 and r[4] - r[5] == 128 and SCRATCH[r[0]][0] != "psum":
                 lst[:] = [e for e in lst if not (r[1] <= e[1] and e[2] <= r[2])]
             lst.append((i, r[1], r[2], w))
         d.discard(i)
@@ -413,14 +506,156 @@ def depend(ops):
     return deps
 
 
-def arrange(ops, deps):
-    nth, place = {}, []
-    for i, o in enumerate(ops):
-        t, key = o[6]
-        nth[o[6]] = nth.get(o[6], -1) + 1
-        x = PERIOD * t + ORDER[key][nth[o[6]]] if key in ORDER else -1000 + i
-        place.append(max([x] + [place[j] + 0.001 for j in deps[i]]))
-    return sorted(range(len(ops)), key=lambda i: (place[i], i))
+def held(o):
+    return o[4] if not o[5] else 1500.0 if o[0] == "g" and o[5] == "dma" else FIX
+
+
+def wait(o, earlier, f):
+    if o[0] == earlier[0] and not earlier[5]:
+        return 0.0 if o[0] == "t" else f["same"]
+    return f["cross"]
+
+
+def first_layout(ops, deps):
+    n = len(ops)
+    after = [[] for _ in ops]
+    for i in range(n):
+        for j in deps[i]:
+            after[j].append(i)
+    due, clock = {}, 0.0
+    for t in range(NV):
+        for step, h in ((1, 0), (1, 1), (2, 0), (2, 1)):
+            clock += GAP["%d%d" % (step, h)]
+            mine = [i for i in range(n) if ops[i][0] == "s" and ops[i][6:9] == (h, "get%d" % step, t)]
+            mine.sort(key=lambda i: any(ops[k][0] == "t" and ops[k][7][:3] == "abs" for k in after[i]))
+            for i in mine + [i for i in range(n) if ops[i][0] == "s" and ops[i][6:9] == (h, "abs%d" % step, t)]:
+                due[i] = clock
+                clock += ops[i][4]
+    clock += GAP["end"]
+    rank = [0.0] * n
+    for i in reversed(range(n)):
+        rank[i] = max([rank[k] + HOP + ops[i][4] for k in after[i]] + [-due.get(i, clock - ops[i][4])])
+    left = [len(d) for d in deps]
+    ready = {i: 0.0 for i in range(n) if not left[i]}
+    free, began, ends = {}, [0.0] * n, [0.0] * n
+    while ready:
+        start = {i: max(s, free.get(ops[i][0], 0.0)) for i, s in ready.items()}
+        first = min(start, key=lambda i: (start[i], -rank[i]))
+        q = ops[first][0]
+        i = max((k for k in ready if ops[k][0] == q and start[k] <= start[first] + LOOK), key=lambda k: (rank[k], -k))
+        del ready[i]
+        began[i], ends[i] = start[i], start[i] + ops[i][4]
+        free[q] = start[i] + FIX if ops[i][5] else ends[i]
+        for k in after[i]:
+            left[k] -= 1
+            if not left[k]:
+                ready[k] = max(ends[j] + (0.0 if ops[j][0] == ops[k][0] == "t" else HOP) for j in deps[k])
+    return began
+
+
+def arrange(ops, deps, others, tries=None, seed=1):
+    n = len(ops)
+    nth, key = {}, []
+    for o in ops:
+        nth[o[6:9]] = nth.get(o[6:9], -1) + 1
+        end = o[8] == NV - 1 and o[7] in ("dec2", "words", "rec", "put", "stock")
+        key.append((o[6], o[7] + "!" * end, nth[o[6:9]]))
+    shift = [1e5 * o[8] for o in ops]
+    q = ["vstgy".index(o[0]) for o in ops]
+    implied = []
+    for i in range(n):
+        implied.append(set(deps[i]).union(*[implied[j] for j in deps[i]]))
+    near = [[j for j in deps[i] if not any(j in implied[k] for k in deps[i])] for i in range(n)]
+    lengths = [([o[4] for o in one], [held(o) for o in one], [[(j, wait(one[i], one[j], f)) for j in near[i]] for i in range(n)])
+               for one, f in zip([ops] + others, FIGURES)]
+    began = first_layout(ops, deps)
+    zero = [min(began[i] for i in range(n) if ops[i][8] == t and ops[i][7] == "get1") for t in range(NV)]
+    x = {}
+    for i in range(n):
+        if ops[i][8] == 1 or key[i] not in x:
+            x[key[i]] = began[i] - zero[ops[i][8]]
+    span = zero[2] - zero[1]
+    shift = [span * o[8] for o in ops]
+
+    def lay(some):
+        place = [-1e9] * n
+        for i in some:
+            p = shift[i] + x[key[i]]
+            for j in near[i]:
+                if place[j] >= p:
+                    p = place[j] + 0.01
+            place[i] = p
+        order = sorted(some, key=lambda i: place[i])
+        total, pairs = 0.0, []
+        for dur, hold, waits in lengths:
+            free, last, end, why = [0.0] * 5, [-1] * 5, [-1e9] * n, [-1] * n
+            for i in order:
+                c = q[i]
+                s, w = free[c], -2 - last[c]
+                for j, h in waits[i]:
+                    if end[j] + h > s:
+                        s, w = end[j] + h, j
+                end[i], free[c], last[c], why[i] = s + dur[i], s + hold[i], i, w
+            total += max(end) / len(lengths)
+            i = end.index(max(end))
+            while why[i] != -1:
+                if why[i] < 0:
+                    pairs.append((-2 - why[i], i))
+                i = why[i] if why[i] >= 0 else -2 - why[i]
+        return total, order, pairs, place
+
+    state = [seed]
+
+    def draw():
+        state[0] = (state[0] * 1103515245 + 12345) % 2147483648
+        return state[0] / 2147483648.0
+
+    def improve(some, tries, ease):
+        keys = list(dict.fromkeys(key[i] for i in some))
+        cur = best = lay(some)
+        kept = dict(x)
+        for it in range(tries):
+            reach = (1.0, 1.0, 300.0, 900.0)[int(4 * draw())] * draw()
+            how, place = draw(), cur[3]
+            if how < 0.7 and cur[2]:
+                a, b = cur[2][int(len(cur[2]) * draw())]
+                if how < 0.3:
+                    move = {key[a]: place[b] - shift[a] + reach}
+                else:
+                    goal = place[a] - reach
+                    move = {key[j]: goal - shift[j] for j in implied[b] if place[j] > goal} if how > 0.5 else {}
+                    move[key[b]] = goal - shift[b]
+            elif how < 0.8:
+                k, step = keys[int(len(keys) * draw())], 3000.0 * (draw() - 0.5)
+                move = {k2: x[k2] + step for k2 in keys if k2[:2] == k[:2]}
+            else:
+                k = keys[int(len(keys) * draw())]
+                move = {k: x[k] + 2400.0 * (draw() - 0.5)}
+            old = {k: x[k] for k in move}
+            x.update(move)
+            new = lay(some)
+            if new[0] <= cur[0] - (5.0 + ease * (1 - it / tries)) * math.log(draw() + 1e-9):
+                cur = new
+                if new[0] < best[0]:
+                    best, kept = new, dict(x)
+            else:
+                x.update(old)
+        x.update(kept)
+        return best[1]
+
+    tries = TRIES if tries is None else tries
+    early = ("addr1", "get1", "abs1", "u", "key1", "dec1", "addr2")
+    middle = [i for i in range(n) if ops[i][8] == 2 or (ops[i][8] == 1 and ops[i][7] not in early) or (ops[i][8] == 3 and ops[i][7] in early)]
+    improve(middle, tries, EASE)
+    for k in x:
+        if k[1][-1] == "!":
+            x[k] = x[(k[0], k[1][:-1], k[2])]
+    order = improve(list(range(n)), tries // 4, EASE / 3)
+    LAID["x"] = (span, dict(x))
+    return order
+
+
+LAID = {}
 
 
 def rank_program(g, core, T, topo):
@@ -432,7 +667,9 @@ def rank_program(g, core, T, topo):
     lanes = len(topo.engines(core, to))
     ops = build(g, T, (rid, pid, topo.mask(core, to)))
     deps = depend(ops)
-    order = arrange(ops, deps)
+    if "order" not in LAID:
+        LAID["order"] = arrange(ops, deps, [], seed=4)
+    order = LAID["order"]
     queue = {"v": g.vector, "s": g.scalar, "t": g.tensor, "g": g, "y": g.sync}
     needed = set(j for i in order for j in deps[i] if not (ops[i][0] == "t" and ops[j][0] == "t"))
     mark, count, nd, far = {}, {q: 0 for q in "vstg"}, 0, 0
@@ -440,7 +677,7 @@ def rank_program(g, core, T, topo):
     pos = {i: n for n, i in enumerate(order)}
     know, direct = {}, {}
     for i in order:
-        q, fn, rd, wr, t, kind, pr = ops[i]
+        q, fn, kind = ops[i][0], ops[i][1], ops[i][5]
         for j in sorted(deps[i], key=lambda j: -pos[j]):
             if j in mark and not (q == "t" and ops[j][0] == "t"):
                 s, n = mark[j]

import math

from concourse.mybir import AluOpType as A, ActivationFunctionType as F

NV = 4
W16 = "float16"
BIG = 8192.0
PLAN = {"10": "p a a a", "11": "a a s s", "20": "a a s s", "21": "v v v s"}
PIECE = {"10": 512, "11": 512, "20": 512, "21": 512}
MASK = "table"
TWO = 1
RUNS = {"10": (0, 4), "11": (0, 4), "20": (0, 4), "21": (0, 3, 4)}
GAP = {"10": 4000.0, "11": 0.0, "20": 1000.0, "21": 2000.0, "end": 7000.0}
LOOK, TRIES, EASE = 150.0, 45000, 150.0

SCRATCH = {
    "X": ("sbuf", [128, 4144], "bfloat16"),
    "XL": ("sbuf", [128, 4096], "bfloat16"),
    "ST": ("sbuf", [128, 3072], "float32"),
    "wdi": ("sbuf", [128, 256], "int32"),
    "pdi": ("sbuf", [128, 1024], "int32"),
    "wti": ("sbuf", [128, 8], "int32"),
    "col": ("sbuf", [128, 16], "float32"),
    "Q": ("sbuf", [128, 16], "bfloat16"),
    "val": ("sbuf", [128, 128], "float32"),
    "gv": ("sbuf", [128, 256], "float32"),
    "CW": ("sbuf", [128, 12 * 128], W16),
    "Ib": ("sbuf", [128, 7 * 128], "bfloat16"),
    "RK": ("sbuf", [128, 56], "bfloat16"),
    "Ci": ("sbuf", [128, 320], "int32"),
    "DZ": ("sbuf", [128, 112], "bfloat16"),
    "TJ": ("sbuf", [128, 2048], "bfloat16"),
    "TP": ("sbuf", [128, 192], "bfloat16"),
    "EL": ("sbuf", [128, 16], "uint16"),
    "STEP": ("sbuf", [128, 392], "float32"),
    "rowf": ("sbuf", [128, 136], "float32"),
    "row": ("sbuf", [128, 1296], "bfloat16"),
}
for _h in range(2):
    for _n, _c, _d in (
        ("F", 2048, "bfloat16"), ("D", 2048, "bfloat16"), ("AD", 2048, "bfloat16"),
        ("O1", 256, "uint16"), ("O2", 256, "uint16"), ("OS", 48, "uint16"),
        ("I", 256, "int32"), ("P", 256, "float32"),
        ("MK", 384, W16), ("B", 128, "float32"), ("OH", 128, "bfloat16"), ("MB", 128, W16),
        ("S1", 408, "float32"), ("S2", 256, "float32"), ("TF", 32, "float32"), ("NF", 136, "float32"), ("SW", 512, "float32"),
        ("TI", 128, "int32"), ("TB", 32, "bfloat16"), ("XE", 320, W16), ("XB", 64, "bfloat16"), ("BASE", 24, W16),
        ("G1", 128, "float32"), ("RI", 128, "int32"),
        ("Wl", NV * 128, W16), ("Wo", NV * 128, W16), ("Yl", 128, "float32"), ("Yo", 128, "float32"),
    ):
        SCRATCH["%s%d" % (_n, _h)] = ("sbuf", [128, _c], _d)
    for _b in range(4):
        SCRATCH["b%d%d" % (_b, _h)] = ("psum", [128, 512], "float32")
SEMAPHORES = ["v", "s", "t", "g", "sent"] + ["d%d" % i for i in range(20)] + ["arr%d" % i for i in range(2 * NV)]

FIX, IND, HOP, DMA, BYTE = 60.0, {"v": 50.0, "s": 65.0}, 150.0, 1200.0, 0.33
FIGURES = [dict(cycle=0.92, gather=1.20, scatter=3.0, pair=1.22, tensor=0.50, v=15.0, s=25.0, t=45.0, psum=45.0, same=155.0, cross=140.0, far=2400.0),
           dict(cycle=0.84, gather=1.07, scatter=2.4, pair=1.25, tensor=0.46, v=10.0, s=20.0, t=55.0, psum=12.0, same=170.0, cross=195.0, far=1900.0),
           dict(cycle=1.15, gather=1.55, scatter=4.2, pair=1.15, tensor=0.50, v=60.0, s=95.0, t=80.0, psum=50.0, same=60.0, cross=170.0, far=2400.0)]


def v(name, lo, hi, st=1, p=128, p0=0):
    return (name, lo, hi, st, p, p0)


def part(x, p0, p):
    return (x[0], x[1], x[2], x[3], p, p0)


def width(x):
    return (x[2] - x[1] + x[3] - 1) // x[3]


def build(g, T, nxt, figures=None):
    f = figures or FIGURES[0]
    CYC, GAT, SCA, PEC, FAR = f["cycle"], f["gather"], f["scatter"], f["tensor"], f["far"]
    ops = []
    now = [0, "const", 0]

    def at(stage):
        now[1] = stage

    def ap(x):
        return T[x[0]][x[5]:x[4], x[1]:x[2]:x[3]] if x[3] > 1 else T[x[0]][x[5]:x[4], x[1]:x[2]]

    def ind(win, off):
        return ap(win).indirect(ap(off))

    def add(q, fn, rd, wr, t, kind=None):
        rd = [r for r in rd if isinstance(r, tuple)]
        if isinstance(t, tuple):
            t = t[0] + (IND[q] if t[1] else f[q]) + (f["psum"] if any(SCRATCH[r[0]][0] == "psum" for r in rd + wr) else 0.0)
        ops.append((q, fn, rd, wr, t, kind, now[0], now[1], now[2]))

    def sc(x):
        return ap(x) if isinstance(x, tuple) else x

    def cost(n, r=1.0):
        return (f["cycle"] * max(64.0, n * r), r > 1.0 and r != 2.0)

    def rate(o, a, off):
        short = all(SCRATCH[x[0]][2] in (W16, "bfloat16", "uint16") for x in (o, a))
        return GAT if off else 0.5 if short else 1.0

    V = g.vector

    def tt(o, a, b, op, off=None):
        two = SCRATCH[a[0]][0] != "psum" and SCRATCH[b[0]][0] != "psum"
        add("v", lambda: V.tensor_tensor(ap(o), ind(a, off) if off else ap(a), ap(b), op), [a, b, off], [o],
            cost(width(o), GAT * f["pair"] if off else 2.0 if two else 1.0))

    def ts(o, a, s1, s2, op0, op1=None, off=None):
        def fn():
            x = ind(a, off) if off else ap(a)
            if op1 is None:
                return V.tensor_scalar(ap(o), x, sc(s1), None, op0)
            return V.tensor_scalar(ap(o), x, sc(s1), sc(s2), op0, op1)
        add("v", fn, [a, s1, s2, off], [o], cost(width(o), rate(o, a, off)))

    def cp(o, a, off=None):
        add("v", lambda: V.tensor_copy(ap(o), ind(a, off) if off else ap(a)), [a, off], [o], cost(width(o), rate(o, a, off)))

    def fill(o, c):
        add("v", lambda: V.memset(ap(o), c), [], [o], cost(width(o)))

    def scan(o, d0, d1, op0, op1):
        add("v", lambda: V.tensor_tensor_scan(ap(o), ap(d0), ap(d1), 0.0, op0, op1), [d0, d1], [o], cost(width(o)))

    def act(o, a, fn, off=None, bias=0.0, scale=1.0):
        add("s", lambda: g.scalar.activation(ap(o), ind(a, off) if off else ap(a), fn, bias=bias, scale=sc(scale)), [a, off, scale], [o],
            cost(width(o), GAT if off else 1.0))

    def mm(group):
        def fn():
            last = None
            for o, l, r, s0, s1 in group:
                last = g.tensor.matmul(ap(o), ap(l), ap(r), s0, s1)
            return last
        t = sum(PEC * max(min(64, width(l)), width(r)) * (4 if SCRATCH[l[0]][2] == "float32" else 1) for o, l, r, s0, s1 in group)
        add("t", fn, [x[1] for x in group] + [x[2] for x in group], [x[0] for x in group], f["t"] + t)

    def acc(terms):
        return [(o, l, r, n == 0, n == len(terms) - 1) for n, (o, l, r) in enumerate(terms)]

    def iota(o, pat, base, cm):
        flt = SCRATCH[o[0]][2] != "int32"
        add("g", (lambda: g.iota(ap(o), pat, base, cm, allow_small_or_imprecise_dtypes=True)) if flt else (lambda: g.iota(ap(o), pat, base, cm)),
            [], [o], 130.0 + 2 * CYC * width(o))

    def dma(q, o, a, rd, wr, row, **kw):
        eng = {"y": g.sync, "s": g.scalar, "g": g}[q]
        add(q, lambda: eng.dma_start(o, a, **kw), rd, wr, DMA + BYTE * row, "dma")

    I16, SM, SP, NL, NR, LF, LG, GG, G3232, G2080, NLM, NRM = [v("CW", 128 * i, 128 * i + 128) for i in range(12)]
    IB, IBM, IB2, IBIG, IBIGM, ONES = [v("Ib", 128 * i, 128 * i + 128) for i in range(6)]
    ZERO = v("Ib", 768, 896)
    ONE, ROW0, ROW1, ROW1B, ROW2, ROW3, ROW4, ROW5 = [v("row", lo, hi, 1, 1) for lo, hi in (
        (0, 128), (128, 264), (264, 536), (536, 672), (672, 800), (800, 1056), (1056, 1184), (1184, 1185))]
    UP, DOWN, FLAT = v("STEP", 0, 128), v("STEP", 128, 263), v("STEP", 264, 392)
    WT, TAU, Ac = v("col", 0, 1), v("col", 4, 5), v("col", 8, 9)
    EL2, EL1 = v("EL", 0, 8), v("EL", 8, 12)
    KEY1, NBR, KEY2, KEY2N, KEY1N, NBRN, WGT = [v("RK", 8 * j, 8 * j + 8) for j in range(7)]

    def diag(j, e):
        return v("DZ", 32 * j + 16 - 16 * e, 32 * j + 48 - 16 * e)

    dma("y", T.wdi[:], T.wd[:], [], [v("wdi", 0, 256)], 1024)
    dma("y", T.X[:, 0:2048], T.xt[:, 0:2048], [], [v("X", 0, 2048)], 8192)
    dma("s", T.X[:, 2048:4096], T.xt[:, 2048:4096], [], [v("X", 2048, 4096)], 8192)
    dma("g", T.wti[:, 0:1], T.wt[:], [], [v("wti", 0, 1)], 3000, allow_slow_non_contiguous=True)
    dma("y", T.pdi[:], T.pd[:], [v("X", 0, 4096)], [v("pdi", 0, 1024)], 4096)

    val, gv, gm = v("val", 0, 128), v("gv", 0, 128), v("gv", 128, 256)
    iota(val, [[-1, 128]], 0, 1)
    ts(I16, val, 0.0, None, A.is_equal)
    ts(SP, val, 1.0, None, A.is_equal)
    ts(v("CW", SP[1] + 15, SP[2], 16), v("val", 15, 128, 16), -15.0, None, A.is_equal)
    ts(NL, SP, 2080.0, None, A.mult)
    ts(NR, I16, 3232.0, None, A.mult)
    tt(LF, NL, NR, A.add)
    ts(NL, SP, 3232.0, None, A.mult)
    ts(NR, I16, 2080.0, None, A.mult)
    tt(LG, NL, NR, A.add)
    for h in range(2):
        ts(v("Wl%d" % h, 0, 128), v("wdi", 128 * h, 128 * h + 128), -2048.0, None, A.add)
    ts(SM, val, -1.0, None, A.is_equal)
    ts(v("CW", SM[1], SM[2], 16), v("val", 0, 128, 16), 15.0, None, A.is_equal)
    tt(NL, SP, I16, A.subtract)
    tt(NR, SM, I16, A.subtract)
    if MASK != "table":
        ts(NLM, NL, -1.0, None, A.mult)
        ts(NRM, NR, -1.0, None, A.mult)
    iota(ZERO, [[0, 128]], 0, 0)
    for o, c in ((IB, 1.0), (IBM, -1.0), (IB2, 2.0), (IBIG, BIG), (IBIGM, -BIG)):
        add("g", lambda o=o, c=c: g.affine_select(ap(o), ap(ZERO), [[-1, 128]], A.not_equal, c, 0, 1), [ZERO], [o], 170.0 + 256 * CYC)
    iota(ONES, [[0, 128]], 1, 0)
    iota(gv, [[-32, 8], [0, 16]], -15, 2)
    act(gv, gv, F.Abs)
    act(gm, gv, F.Sign, bias=16.0, scale=-1.0)
    act(gm, gm, F.Relu)
    cp(GG, gm)
    ts(G3232, gm, 3232.0, None, A.mult)
    ts(G2080, gm, 2080.0, None, A.mult)
    g8 = v("gv", 128, 256, 16)
    cp(WT, v("wti", 0, 1))
    for o, c in ((KEY1, -2048.0), (KEY1N, 2048.0), (NBR, 2.0 ** -12), (NBRN, -2.0 ** -12), (KEY2, -4096.0), (KEY2N, 4096.0), (WGT, WT)):
        act(o, g8, F.Identity, scale=c)
    iota(v("Ci", 128, 256), [[0, 8], [-1, 16]], 16, 1)
    iota(v("Ci", 256, 320), [[1, 16], [1, 4]], 15, 1)
    ts(v("Ci", 128, 320), v("Ci", 128, 320), 15, None, A.bitwise_and)
    ts(v("TJ", 0, 128), v("Ci", 128, 256), 0.0, None, A.is_equal)
    for j, c in enumerate((0.0, 15.0, 1.0)):
        ts(v("TP", 64 * j, 64 * j + 64), v("Ci", 256, 320), c, None, A.is_equal)
    iota(v("DZ", 0, 112), [[0, 112]], 0, 0)
    for j, c in enumerate((1.0, 1024.0, 128.0)):
        act(v("DZ", 32 * j + 16, 32 * j + 32), v("TJ", 0, 16), F.Identity, scale=c)
    for n in (128, 256, 512, 1024):
        dma("y", T.TJ[:, n:2 * n], T.TJ[:, 0:n], [v("TJ", 0, n)], [v("TJ", n, 2 * n)], 2 * n)
    P_, C0, CC, R8, X2, X1 = v("Ci", 80, 81), v("Ci", 81, 82), v("Ci", 82, 83), v("Ci", 83, 84), v("Ci", 88, 96), v("Ci", 96, 100)
    iota(P_, [[0, 1]], 0, 1)
    ts(C0, P_, 4, None, A.arith_shift_right)
    ts(CC, P_, 7, None, A.bitwise_and)
    ts(R8, P_, 8, None, A.bitwise_and)
    tt(v("col", 1, 2), C0, CC, A.is_equal)
    cp(v("col", 2, 3), R8)
    ts(v("col", 3, 4), R8, 0.125, None, A.mult)
    iota(X2, [[1, 8]], -24, 0)
    iota(X1, [[2, 4]], -24, 0)
    ts(X2, X2, v("col", 2, 3), v("col", 1, 2), A.add, A.mult)
    ts(X1, X1, v("col", 3, 4), v("col", 1, 2), A.add, A.mult)
    ts(v("EL", 0, 12), v("Ci", 88, 100), 24.0, None, A.add)
    iota(TAU, [[0, 1]], 15 if TWO else -17, 16)
    for h in range(2 * TWO):
        iota(v("TF%d" % h, 0, 32), [[0, 32]], -15, -16)
    iota(UP, [[0, 128]], 1, 0)
    iota(v("STEP", 0, 128, 16), [[0, 8]], 1 - 2 ** 24, 0)
    if TWO:
        ts(FLAT, UP, -1.0, None, A.add)
    iota(DOWN, [[0, 135]], -1, 0)
    iota(v("STEP", 128, 263, 17), [[0, 8]], 2 ** 24 - 1, 0)
    r15 = v("rowf", 0, 136, 1, 1)
    iota(r15, [[0, 8], [-1, 17]], 15, 0)
    iota(ONE, [[0, 128]], 1, 0)
    act(ROW0, r15, F.Relu, scale=1048576.0)
    act(v("row", 264, 400, 1, 1), r15, F.Identity, scale=0.0)
    act(v("row", 400, 536, 1, 1), r15, F.Relu, bias=1.5, scale=4.0)
    act(ROW1B, r15, F.Identity, bias=2.0 ** -13, scale=0.0)
    iota(ROW2, [[0, 128]], -32, 0)
    iota(ROW3, [[1152, 2], [0, 128]], 2080, 0)
    iota(ROW4, [[0, 128]], -int(BIG), 0)
    iota(ROW5, [[0, 1]], 5120, 0)
    TL = v("Ci", 104, 112)
    iota(TL, [[0, 8]], 0, 1)
    ts(TL, TL, 15, None, A.bitwise_and)
    iota(v("Ci", 112, 120), [[16, 8]], 0, 0)
    tt(TL, TL, v("Ci", 112, 120), A.add)
    for h in range(2):
        ts(v("BASE%d" % h, 0, 8), TL, 16.0, None, A.mult)
        ts(v("BASE%d" % h, 8, 16), TL, 4.0, 512.0 * h, A.mult, A.add)
        cp(v("BASE%d" % h, 16, 24), TL)
        iota(v("TI%d" % h, 0, 128), [[0, 128]], 0, 0)
        iota(v("TB%d" % h, 0, 32), [[0, 32]], 0, 0)
    cp(v("ST", 0, 1024), v("pdi", 0, 1024))
    for n in (1024, 2048):
        dma("y", T.ST[:, n:n + 1024], T.ST[:, 0:1024], [v("ST", 0, 1024)], [v("ST", n, n + 1024)], 4096)

    def names(h):
        return lambda n, lo, hi, st=1: v("%s%d" % (n, h), lo, hi, st)

    def numbers(o, i, t):
        if t:
            ts(o, i, Ac, None, A.subtract)
        else:
            cp(o, i)

    def gathers(t, h, step):
        u = names(h)
        Xw = v("X", 0, 4128 if t else 4096)
        off, n = "O%d" % step, 0
        hi = 0
        for piece in PLAN["%d%d" % (step, h)].split():
            who, lo, hi = piece[0], hi, hi + 512 * len(piece)
            o1, o2 = u(off, lo // 16, hi // 16), u(off, 128 + lo // 16, 128 + hi // 16)
            at("get%d" % step)
            if who in "sp":
                act(u("F", lo, hi), Xw, F.Identity, off=o1, scale=1.0 / step)
                if who == "s":
                    act(u("D", lo, hi), Xw, F.Copy, off=o2)
                else:
                    cp(u("D", lo, hi), Xw, off=o2)
                at("abs%d" % step)
                for s in range(lo, hi, 512):
                    bank = u("b3" if n % 2 == 0 else "b0", 0, 512)
                    n += 1
                    mm(acc([(bank, IB if step == 1 else IB2, u("F", s, s + 512)), (bank, IBM, u("D", s, s + 512))]))
                    act(u("AD", s, s + 512), bank, F.Abs)
            else:
                act(u("F", lo, hi), Xw, F.Copy, off=o1)
                w = PIECE["%d%d" % (step, h)]
                for s in range(lo, hi, w):
                    tt(u("D", s, s + w), Xw, u("F", s, s + w), A.subtract, off=u(off, 128 + s // 16, 128 + (s + w) // 16))
                at("abs%d" % step)
                if who == "a":
                    act(u("AD", lo, hi), u("D", lo, hi), F.Abs)
                else:
                    ts(u("AD", lo, hi), u("D", lo, hi), 0.0, 2.0, A.max, A.mult)

    def runs(h, step):
        key = "%d%d" % (step, h)
        u = names(h)
        for a, b in zip(RUNS[key], RUNS[key][1:]):
            lo, hi = 512 * a, 512 * b
            form = set(c == "v" for c in PLAN[key].replace(" ", "")[a:b])
            assert len(form) == 1
            dist = [[u(n, lo + k, hi, 16) for k in range(16)] for n in (("D", "AD") if True in form else ("AD",))]
            yield 32 * a, 32 * b, dist, [u("F", lo + k, hi, 16) for k in range(16)]

    def spread(terms, base=None):
        out = []
        for a in range(4):
            first = [(part(base[0], 32 * a, 32 * a + 32), v("CW", 32 * a, 32 * a + 32), base[1])] if base else []
            out += acc(first + [(part(o, 32 * a, 32 * a + 32), diag(j, e), v(x[0], x[1] + n * (2 * a + e), x[1] + n * (2 * a + e + 1)))
                                for o, x, n, j in terms for e in range(2)])
        return out

    def step1(t, h):
        u = names(h)
        W = u("Wl", 128 * t, 128 * t + 128)
        at("addr1")
        mm([(u("b0", 0, 128), SP, W, True, True), (u("b0", 128, 256), LF, W, True, True), (u("b0", 256, 384), LG, W, True, True)])
        tt(u("P", 0, 128), u("b0", 0, 128), W, A.mult)
        tt(u("I", 0, 128), u("b0", 128, 256), u("P", 0, 128), A.add)
        tt(u("I", 128, 256), u("b0", 256, 384), u("P", 0, 128), A.add)
        for lo, hi in ((0, 128), (128, 256)) if h else ((0, 256),):
            ts(u("I", lo, hi), u("I", lo, hi), 5, 4095, A.arith_shift_right, A.bitwise_and)
        for lo, hi in ((0, 128), (128, 256)):
            numbers(u("O1", lo, hi), u("I", lo, hi), t)
        gathers(t, h, 1)
        for p0, p1, dist, first in runs(h, 1):
            def out(bank, lo, hi, st=1):
                return part(u(bank, lo, hi, st), p0, p1)
            one = v("row", 0, p1 - p0, 1, 1)
            at("u")
            mm(acc([(out("b2", 0, 136), one, ROW0)] + [(out("b2", k, 136, 17), first[k], WGT) for k in range(16)]))
            at("key1")
            terms = [(out("b1", 0, 272), one, ROW1), (out("b1", 136, 272), one, ROW1B)]
            for s, d in enumerate(dist):
                w = 32 * (s < len(dist) - 1)
                terms += [(out("b1", k + 1, 272, 17), d[k], v("RK", w, w + 16)) for k in range(15)]
                terms += [(out("b1", 16, 136, 17), d[15], v("RK", w, w + 8)), (out("b1", 136, 272, 17), d[15], v("RK", w + 8, w + 16))]
                terms += [(out("b1", 136 + (k - 1) % 16, 272, 17), d[k], v("RK", 40 - w, 48 - w)) for k in range(16)]
            terms = acc(terms)
            mm(terms[:-33])
            mm(terms[-33:])
        at("dec1")
        scan(u("S1", 272, 407), DOWN, u("b1", 1, 136), A.add, A.min)
        tt(u("NF", 0, 135), u("b1", 1, 136), u("S1", 272, 407), A.not_equal)
        scan(u("S1", 0, 135), u("NF", 0, 135), u("b2", 0, 135), A.mult, A.max)
        scan(u("S1", 136, 271), u("NF", 0, 135), u("b1", 136, 271), A.mult, A.max)
        cp(u("TI", 0, 16), u("S1", 15, 272, 17))
        ts(u("TI", 32, 48), u("TI", 0, 16), 1023, None, A.bitwise_and)
        cp(u("XE", 0, 128), u("TI", 32, 64), off=EL2)
        mm(spread([(u("b1", 288, 304), u("XE", 0, 128), 16, 0)]))
        cp(u("OS", 0, 16), u("b1", 288, 304))
        act(u("B", 0, 128), v("ST", 0, 1024), F.Identity, off=u("OS", 0, 8), bias=-2048.0)

    def step2(t, h):
        u = names(h)
        W = u("Wl", 128 * t, 128 * t + 128)
        ma, mb, mp = u("MK", 0, 128), u("MK", 128, 256), u("MK", 256, 384)
        OH, B = u("OH", 0, 128), u("B", 0, 128)
        at("addr2")
        act(OH, v("TP", 0, 64), F.Copy, off=u("OS", 8, 16))
        if MASK != "table":
            mm([(u("b2", 136, 264), SM, W, True, True), (u("b2", 264, 392), SP, W, True, True)])
        for j, (bank, m, lin) in enumerate((("b0", ma, G3232), ("b3", mb, G2080))):
            lo, hi = 128 * j, 128 * j + 128
            both = acc([(u(bank, 0, 128), ONE, v("row", ROW3[1] + lo, ROW3[1] + hi, 1, 1)), (u(bank, 0, 128), GG, m)])
            mm(both[:1])
            if MASK == "table":
                tt(m, v("TP", 64 + 64 * j, 128 + 64 * j), W, A.mult, off=u("OS", 8, 16))
            else:
                tt(m, u("b2", 136 + lo, 136 + hi), OH, A.mult)
            mm(both[1:] + [(u(bank, 128, 256), lin, m, True, True)])
            tt(u("P", lo, hi), u(bank, 0, 128), B, A.mult)
            tt(u("I", lo, hi), u(bank, 128, 256), u("P", lo, hi), A.add)
            ts(u("I", lo, hi), u("I", lo, hi), 5, 4095, A.arith_shift_right, A.bitwise_and)
            numbers(u("O2", lo, hi), u("I", lo, hi), t)
        at("side")
        mm([(u("b2", 0, 128), I16, W, True, True)])
        tt(mp, u("b2", 0, 128), OH, A.mult)
        if MASK == "table":
            left, right = [(NR, ma), (NL, mp)], [(NL, mb), (NR, mp)]
        else:
            left, right = [(NLM, ma), (NL, mp)], [(NRM, mb), (NR, mp)]
        mm(acc([(u("b2", 0, 128), l, r) for l, r in [(I16, W)] + left]) + acc([(u("b2", 128, 256), l, r) for l, r in [(I16, W)] + right]) +
           acc([(u("b2", 256, 384), I16, W), (u("b2", 256, 384), IBIGM, OH)]))
        act(u("SW", 128, 512), u("b2", 0, 384), F.Copy)
        ts(u("TI", 64, 72), u("TI", 32, 40), 15, None, A.bitwise_and)
        ts(u("TI", 72, 88), u("TI", 32, 48), 3, None, A.bitwise_and)
        cp(u("XE", 128, 256), u("TI", 64, 96), off=EL2)
        gathers(t, h, 2)
        for p0, p1, dist, first in runs(h, 2):
            at("key2")
            key = acc([(part(u("b1", 0, 128), p0, p1), v("row", 0, p1 - p0, 1, 1), ROW2)] +
                      [(part(u("b1", k, 128, 16), p0, p1), d[k], (KEY2N, KEY2)[s == len(dist) - 1]) for s, d in enumerate(dist) for k in range(16)])
            mm(key[:17])
            if len(dist) == 2:
                mm(key[17:])
        at("dec2")
        scan(u("S2", 0, 128), UP, u("b1", 0, 128), A.add, A.max)
        if TWO:
            scan(u("S2", 128, 256), FLAT, u("b1", 0, 128), A.add, A.max)
        last = u("S2", 15, 128, 16)
        tt(u("TB", 8, 16), last, u("S1", 272 + 15, 407, 17), A.is_lt)
        if t < NV - 1:
            at("count")
            c = u("b3", 0, 1)
            mm(acc(([(c, ONE, ROW5)] if h == 0 else []) + [(c, ONES, u("TB", 8 + j, 9 + j)) for j in range(8)]))
            at("dec2")
        if TWO:
            tt(u("TF", 0, 8), u("S2", 128 + 15, 256, 16), last, A.subtract)
            ts(u("XE", 256, 320), u("TF", 0, 32), TAU, None, A.add, off=EL1)
        else:
            ts(u("TI", 16, 24), last, -1.0, TAU, A.mult, A.add)
            ts(u("TI", 96, 104), u("TI", 16, 24), 4095, None, A.bitwise_and)
            cp(u("XE", 256, 320), u("TI", 96, 128), off=EL1)
        mm(spread([(u("b1", 256, 264), u("XE", 256, 320), 8, 0)]))
        slot = u("OS", 16, 24)
        cp(slot, u("b1", 256, 264))
        at("words")
        tt(u("MB", 0, 128), v("TJ", 0, 2048), B, A.mult, off=slot)
        mm(acc([(u("b0", 0, 128), ONE, ROW4), (u("b0", 0, 128), IBIG, OH), (u("b0", 0, 128), GG, u("MB", 0, 128))]))
        tt(u("SW", 0, 128), u("b0", 0, 128), u("SW", 384, 512), A.max)
        tt(u("TB", 0, 8), u("TB", 8, 16), u("TI", 80, 88), A.mult)
        act(u("XB", 0, 64), u("TB", 0, 32), F.Copy, off=EL1)
        mm(spread([(u("b2", 384, 400), u("XE", 128, 256), 16, 0), (u("b2", 392, 400), u("XB", 0, 64), 8, 1),
                   (u("b2", 400, 408), u("XB", 0, 64), 8, 2)], (u("b2", 384, 408), u("BASE", 0, 24))))
        cp(u("OS", 24, 48), u("b2", 384, 408))
        at("rec")
        act(u("G1", 0, 128), u("D", 0, 2048), F.Identity, off=slot, bias=-0.25, scale=0.5)
        tt(u("RI", 0, 128), u("F", 0, 2048), u("G1", 0, 128), A.add, off=slot)
        at("words")
        if t < NV - 1:
            src, dst = u("Wo", 128 * t, 128 * t + 128), u("Wl", 128 * t + 128, 128 * t + 256)
            act(src, u("SW", 0, 384), F.Copy, off=u("OS", 40, 48))
        else:
            src, dst = u("Yo", 0, 128), u("Yl", 0, 128)
            act(src, u("SW", 0, 384), F.Identity, off=u("OS", 40, 48), bias=2048.0)
        sem = T.sem["arr%d" % (2 * t + h)]
        add("g", lambda: g.remote_dma(ap(dst), ap(src), sem, T.sem.sent, nxt[1], nxt[0], nxt[2]), [src], [dst], FAR, ("far", "arr%d" % (2 * t + h)))

    def writes(t, h):
        u = names(h)
        at("put")
        xw, o = v("X" if t < NV - 1 else "XL", 2048 * h, 2048 * h + 2048), u("OS", 24, 32)
        add("v", lambda: V.tensor_copy(ind(xw, o), ap(u("RI", 0, 128))), [o, u("RI", 0, 128)], [xw], cost(128, SCA))
        if h == 0 and t < NV - 1:
            at("wrap")
            act(v("X", 4096, 4128), v("X", 0, 32), F.Copy)
        at("stock")
        sw, o2 = v("ST", 0, 3072), u("OS", 32, 40)
        add("v", lambda: V.tensor_scalar(ind(sw, o2), ap(u("SW", 0, 128)), 1.0, 2048.0, A.mult, A.add), [o2, u("SW", 0, 128)], [sw], cost(128, SCA))
        if t == NV - 1:
            at("out")
            lo, hi = 2048 * h, 2048 * h + 2048
            dma("y", T.yx[:, lo:hi], T.XL[:, lo:hi], [v("XL", lo, hi)], [], 4096)
            dma("s" if h else "y", T.yp[:, 512 * h:512 * h + 512], T.ST[:, 512 * h:512 * h + 512], [v("ST", 512 * h, 512 * h + 512)], [], 2048)
            dma("y", T.yw[:, 128 * h:128 * h + 128], T["Yl%d" % h][:], [v("Yl%d" % h, 0, 128)], [], 512)

    for t in range(NV):
        now[2] = t
        if t == NV - 1:
            at("keep")
            dma("y", T.XL[:], T.X[:, 0:4096], [v("X", 0, 4096)], [v("XL", 0, 4096)], 8192)
        for step in (step1, step2, writes):
            for h in range(2):
                now[0] = h
                step(t, h)
        if t < NV - 1:
            at("count")
            c0, c1, Q = v("b30", 0, 1), v("b31", 0, 1), v("Q", 0, 1)
            ts(Q, c1, c0, -15.5, A.add, A.add)
            ts(Ac, Q, c0, c1, A.subtract, A.subtract)
        now[0] = 0
    return ops


def depend(ops):
    seen = {}
    deps = []
    for i, o in enumerate(ops):
        d = set()
        acc = [(r, False) for r in o[2]] + [(r, True) for r in o[3]]
        for r, w in acc:
            ps = SCRATCH[r[0]][0] == "psum"
            for j, lo, hi, w2 in seen.get(r[0], []):
                if (ps and (ops[j][0] != o[0] or o[0] == "t")) or ((w or w2) and lo < r[2] and r[1] < hi):
                    d.add(j)
        for r, w in acc:
            lst = seen.setdefault(r[0], [])
            if w and r[3] == 1 and r[4] - r[5] == 128 and SCRATCH[r[0]][0] != "psum":
                lst[:] = [e for e in lst if not (r[1] <= e[1] and e[2] <= r[2])]
            lst.append((i, r[1], r[2], w))
        d.discard(i)
        deps.append(sorted(d))
    return deps


def held(o):
    return o[4] if not o[5] else 1500.0 if o[0] == "g" and o[5] == "dma" else FIX


def wait(o, earlier, f):
    if o[0] == earlier[0] and not earlier[5]:
        return 0.0 if o[0] == "t" else f["same"]
    return f["cross"]


def first_layout(ops, deps):
    n = len(ops)
    after = [[] for _ in ops]
    for i in range(n):
        for j in deps[i]:
            after[j].append(i)
    due, clock = {}, 0.0
    for t in range(NV):
        for step, h in ((1, 0), (1, 1), (2, 0), (2, 1)):
            clock += GAP["%d%d" % (step, h)]
            mine = [i for i in range(n) if ops[i][0] == "s" and ops[i][6:9] == (h, "get%d" % step, t)]
            mine.sort(key=lambda i: any(ops[k][0] == "t" and ops[k][7][:3] == "abs" for k in after[i]))
            for i in mine + [i for i in range(n) if ops[i][0] == "s" and ops[i][6:9] == (h, "abs%d" % step, t)]:
                due[i] = clock
                clock += ops[i][4]
    clock += GAP["end"]
    rank = [0.0] * n
    for i in reversed(range(n)):
        rank[i] = max([rank[k] + HOP + ops[i][4] for k in after[i]] + [-due.get(i, clock - ops[i][4])])
    left = [len(d) for d in deps]
    ready = {i: 0.0 for i in range(n) if not left[i]}
    free, began, ends = {}, [0.0] * n, [0.0] * n
    while ready:
        start = {i: max(s, free.get(ops[i][0], 0.0)) for i, s in ready.items()}
        first = min(start, key=lambda i: (start[i], -rank[i]))
        q = ops[first][0]
        i = max((k for k in ready if ops[k][0] == q and start[k] <= start[first] + LOOK), key=lambda k: (rank[k], -k))
        del ready[i]
        began[i], ends[i] = start[i], start[i] + ops[i][4]
        free[q] = start[i] + FIX if ops[i][5] else ends[i]
        for k in after[i]:
            left[k] -= 1
            if not left[k]:
                ready[k] = max(ends[j] + (0.0 if ops[j][0] == ops[k][0] == "t" else HOP) for j in deps[k])
    return began


def arrange(ops, deps, others, tries=None, seed=1):
    n = len(ops)
    nth, key = {}, []
    for o in ops:
        nth[o[6:9]] = nth.get(o[6:9], -1) + 1
        end = o[8] == NV - 1 and o[7] in ("dec2", "words", "rec", "put", "stock")
        key.append((o[6], o[7] + "!" * end, nth[o[6:9]]))
    shift = [1e5 * o[8] for o in ops]
    q = ["vstgy".index(o[0]) for o in ops]
    implied = []
    for i in range(n):
        implied.append(set(deps[i]).union(*[implied[j] for j in deps[i]]))
    near = [[j for j in deps[i] if not any(j in implied[k] for k in deps[i])] for i in range(n)]
    lengths = [([o[4] for o in one], [held(o) for o in one], [[(j, wait(one[i], one[j], f)) for j in near[i]] for i in range(n)])
               for one, f in zip([ops] + others, FIGURES)]
    began = first_layout(ops, deps)
    zero = [min(began[i] for i in range(n) if ops[i][8] == t and ops[i][7] == "get1") for t in range(NV)]
    x = {}
    for i in range(n):
        if ops[i][8] == 1 or key[i] not in x:
            x[key[i]] = began[i] - zero[ops[i][8]]
    span = zero[2] - zero[1]
    shift = [span * o[8] for o in ops]

    def lay(some):
        place = [-1e9] * n
        for i in some:
            p = shift[i] + x[key[i]]
            for j in near[i]:
                if place[j] >= p:
                    p = place[j] + 0.01
            place[i] = p
        order = sorted(some, key=lambda i: place[i])
        total, pairs = 0.0, []
        for dur, hold, waits in lengths:
            free, last, end, why = [0.0] * 5, [-1] * 5, [-1e9] * n, [-1] * n
            for i in order:
                c = q[i]
                s, w = free[c], -2 - last[c]
                for j, h in waits[i]:
                    if end[j] + h > s:
                        s, w = end[j] + h, j
                end[i], free[c], last[c], why[i] = s + dur[i], s + hold[i], i, w
            total += max(end) / len(lengths)
            i = end.index(max(end))
            while why[i] != -1:
                if why[i] < 0:
                    pairs.append((-2 - why[i], i))
                i = why[i] if why[i] >= 0 else -2 - why[i]
        return total, order, pairs, place

    state = [seed]

    def draw():
        state[0] = (state[0] * 1103515245 + 12345) % 2147483648
        return state[0] / 2147483648.0

    def improve(some, tries, ease):
        keys = list(dict.fromkeys(key[i] for i in some))
        cur = best = lay(some)
        kept = dict(x)
        for it in range(tries):
            reach = (1.0, 1.0, 300.0, 900.0)[int(4 * draw())] * draw()
            how, place = draw(), cur[3]
            if how < 0.7 and cur[2]:
                a, b = cur[2][int(len(cur[2]) * draw())]
                if how < 0.3:
                    move = {key[a]: place[b] - shift[a] + reach}
                else:
                    goal = place[a] - reach
                    move = {key[j]: goal - shift[j] for j in implied[b] if place[j] > goal} if how > 0.5 else {}
                    move[key[b]] = goal - shift[b]
            elif how < 0.8:
                k, step = keys[int(len(keys) * draw())], 3000.0 * (draw() - 0.5)
                move = {k2: x[k2] + step for k2 in keys if k2[:2] == k[:2]}
            else:
                k = keys[int(len(keys) * draw())]
                move = {k: x[k] + 2400.0 * (draw() - 0.5)}
            old = {k: x[k] for k in move}
            x.update(move)
            new = lay(some)
            if new[0] <= cur[0] - (5.0 + ease * (1 - it / tries)) * math.log(draw() + 1e-9):
                cur = new
                if new[0] < best[0]:
                    best, kept = new, dict(x)
            else:
                x.update(old)
        x.update(kept)
        return best[1]

    tries = TRIES if tries is None else tries
    early = ("addr1", "get1", "abs1", "u", "key1", "dec1", "addr2")
    middle = [i for i in range(n) if ops[i][8] == 2 or (ops[i][8] == 1 and ops[i][7] not in early) or (ops[i][8] == 3 and ops[i][7] in early)]
    improve(middle, tries, EASE)
    for k in x:
        if k[1][-1] == "!":
            x[k] = x[(k[0], k[1][:-1], k[2])]
    order = improve(list(range(n)), tries // 4, EASE / 3)
    LAID["x"] = (span, dict(x))
    return order


LAID = {}


def rank_program(g, core, T, topo):
    rank = T.rank_of(core)
    if rank is None:
        return
    to = T.cores[(rank + 1) % len(T.cores)]
    rid, pid = topo.addr(to)[0:2]
    lanes = len(topo.engines(core, to))
    ops = build(g, T, (rid, pid, topo.mask(core, to)))
    deps = depend(ops)
    if "order" not in LAID:
        LAID["order"] = arrange(ops, deps, [], seed=4)
    order = LAID["order"]
    queue = {"v": g.vector, "s": g.scalar, "t": g.tensor, "g": g, "y": g.sync}
    needed = set(j for i in order for j in deps[i] if not (ops[i][0] == "t" and ops[j][0] == "t"))
    mark, count, nd, far = {}, {q: 0 for q in "vstg"}, 0, 0
    waited = {q: {} for q in queue}
    pos = {i: n for n, i in enumerate(order)}
    know, direct = {}, {}
    for i in order:
        q, fn, kind = ops[i][0], ops[i][1], ops[i][5]
        for j in sorted(deps[i], key=lambda j: -pos[j]):
            if j in mark and not (q == "t" and ops[j][0] == "t"):
                s, n = mark[j]
                if waited[q].get(s, 0) < n:
                    queue[q].wait_ge(T.sem[s], n)
                    waited[q][s] = n
                    direct[s] = max(direct.get(s, 0), n)
                    for s2, n2 in know[j].items():
                        waited[q][s2] = max(waited[q].get(s2, 0), n2)
        know[i] = dict(waited[q]) if kind is None or kind == "dma" else {}
        x = fn()
        if kind == "dma":
            mark[i] = ("d%d" % nd, 16)
            x.then_inc(T.sem["d%d" % nd], 16)
            nd += 1
        elif kind is not None:
            mark[i] = (kind[1], lanes)
            far += 1
        elif i in needed:
            count[q] += 1
            mark[i] = (q, count[q])
            x.then_inc(T.sem[q], 1)
    g.wait_ge(T.sem.sent, far * lanes)
    last = {}
    for s, n in mark.values():
        last[s] = max(last.get(s, 0), n)
    for s in last:
        if direct.get(s, 0) < last[s]:
            g.wait_ge(T.sem[s], last[s])
